import numpy as np, ml_dtypes
CORES = [9,25,41,57]
N = 4
BF = ml_dtypes.bfloat16
X, Y, n, ORD = 64, 64, 64, 3
def normal(rng, *shape):
    v = rng.standard_normal(shape, dtype=np.float32)
    return np.where(v < 0, np.float32(-1), np.float32(1)) * np.clip(np.abs(v), np.float32(2.0 ** -8), np.float32(3))
def setup_inputs(rng):
    q = normal(rng, N, 128, n) * np.exp2(rng.integers(-1, 2, (N, 128, 1))).astype(np.float32)
    refl = ((0.5 + rng.random((N, 128, n))) * 2.0 ** -4 * rng.choice(np.array([-1.0, 1.0]), (N, 128, n))).astype(np.float32)
    return {"px": rng.integers(0, X, (N, 8, n)).astype(np.int32), "py": rng.integers(0, Y, (N, 8, n)).astype(np.int32), "q": q.astype(np.float32), "refl": refl,
            "green": normal(rng, N, 128, X * Y).astype(BF)}
def setup_inputs_corners(rng):
    d = setup_inputs(rng)
    d["px"] = rng.choice(np.array([0, 1, X - 2, X - 1]), (N, 8, n)).astype(np.int32); d["py"] = rng.choice(np.array([0, 1, Y - 2, Y - 1]), (N, 8, n)).astype(np.int32)
    d["px"][:, :, 0] = 0; d["py"][:, :, 0] = 0; d["px"][:, :, n - 1] = X - 1; d["py"][:, :, n - 1] = Y - 1; return d
def setup_inputs_lines(rng):
    d = setup_inputs(rng)
    for g in range(8):
        if g % 2 == 0: d["px"][:, g] = rng.integers(0, X)
        else: d["py"][:, g] = rng.integers(0, Y)
    return d
def setup_inputs_heap(rng):
    d = setup_inputs(rng)
    for g in range(8):
        r = int(rng.integers(0, N)); t = (r + 1 + int(rng.integers(0, N - 1))) % N; u = (t + 1) % N
        if u == r: u = (u + 1) % N
        d["px"][r, g] = rng.integers(0, X); d["py"][r, g] = rng.integers(0, Y)
        d["px"][t, g] = d["px"][u, g]; d["py"][t, g] = d["py"][u, g]
    return d
def setup_inputs_lamp(rng):
    d = setup_inputs(rng); keep = np.zeros((N, 8), np.float32); keep[rng.integers(0, N, 8), np.arange(8)] = 1
    d["q"] = d["q"] * np.repeat(keep, 16, axis=1)[:, :, None]; d["refl"] = d["refl"] * (rng.random((N, 1, n)) < 0.5).astype(np.float32); return d
def setup_inputs_spread(rng):
    d = setup_inputs(rng); z = np.exp2(rng.integers(-6, 7, (N, 1, n))) * (rng.random((N, 1, n)) > 0.0625)
    d["q"] = (d["q"] * z).astype(np.float32); d["refl"] = d["refl"] * np.float32(2.0 ** -5)
    c = (np.exp2(rng.integers(-6, 7, (N, 1, X * Y))) * (rng.random((N, 1, X * Y)) > 0.0625)).astype(np.float32); s = np.exp2(rng.integers(-2, 2, (N, 128, 1))).astype(np.float32)
    d["green"] = (d["green"].astype(np.float32) * s * c).astype(BF); return d
def check_inputs(d):
    bad = []
    if not ((d["px"] >= 0) & (d["px"] < X)).all(): bad.append("px_range")
    if not ((d["py"] >= 0) & (d["py"] < Y)).all(): bad.append("py_range")
    for k in ("q", "refl", "green"):
        if not np.isfinite(d[k].astype(np.float32)).all(): bad.append(k + "_finite")
    return bad
def reference(px, py, q, refl, green):
    y = np.zeros((N, 128, n), np.float64); own = np.arange(n)
    for g in range(8):
        p = slice(16 * g, 16 * g + 16)
        cx = px[:, g].astype(np.int64).reshape(-1); cy = py[:, g].astype(np.int64).reshape(-1)
        off = np.abs(cx[:, None] - cx[None, :]) * Y + np.abs(cy[:, None] - cy[None, :])
        parts = []
        for s in range(N):
            m = green[s, p].astype(np.float64)[:, off[:, s * n:(s + 1) * n]]; m[:, s * n + own, own] = 0
            parts.append(m)
        M = np.concatenate(parts, axis=2)
        w = q[:, p].astype(np.float64).transpose(1, 0, 2).reshape(16, N * n); a = refl[:, p].astype(np.float64).transpose(1, 0, 2).reshape(16, N * n)
        total = np.zeros((16, N * n), np.float64)
        for o in range(ORD):
            fd = np.matmul(M, w[:, :, None])[:, :, 0]
            total = total + fd; w = a * fd
        y[:, p] = total.reshape(16, N, n).transpose(1, 0, 2)
    return {"y": y.astype(np.float32)}

@@ -1,0 +1,371 @@
+from concourse.bass import DstId, RemoteDMATransfer
+from concourse.mybir import AluOpType, ActivationFunctionType
+
+NR = 4
+F32, BF = "float32", "bfloat16"
+SPLAN = [("gather", 0, 0, 2), ("gather", 0, 2, 3), ("places", 1, 1, 2), ("places", 2, 2, 4), ("gather", 1, 2, 6), ("gather", 2, 0, 5),
+         ("gather", 3, 3, 8), ("gather", 3, 0, 3), ("gather", 0, 5, 8)]
+VPLAN = [("gather", 0, 3, 5), ("places", 1, 1, 2), ("turn", 0, 0, 3), ("offsets", 1, 1, 2), ("list", 1, 1, 2), ("places", 2, 2, 4),
+         ("offsets", 2, 2, 4), ("gather", 1, 0, 2), ("list", 2, 2, 4), ("gather", 1, 6, 8), ("turn", 0, 3, 5), ("turn", 1, 0, 8),
+         ("gather", 2, 5, 8), ("turn", 2, 0, 5), ("turn", 2, 5, 8), ("turn", 3, 4, 8), ("evac", 1, 0, 0), ("evac", 1, 1, 0),
+         ("turn", 3, 0, 4), ("evac", 3, 0, 0), ("turn", 0, 5, 8), ("evac", 3, 1, 0)]
+COPIERS = {"12": ["gv", "gv"], "3": "vv", "fb": ["vs", "vs"], "fa": ["vs", "vs"]}
+SCRATCH = {
+    "Gt": ("sbuf", [128, 4096], BF),
+    "Mg": ("sbuf", [128, 16384], BF),
+    "Tt": ("sbuf", [128, 16384], BF),
+    "OFF": ("sbuf", [128, 1024], "uint16"),
+    "DX": ("sbuf", [128, 4, 64, 4], BF), "RA": ("sbuf", [128, 4, 64, 4], BF),
+    "C8i": ("sbuf", [128, 128], "int32"), "C8b": ("sbuf", [128, 128], BF),
+    "SCf": ("sbuf", [128, 12], F32),
+    "CLT": ("sbuf", [128, 4, 128], BF),
+    "ONB": ("sbuf", [128, 144], BF), "ONF": ("sbuf", [128, 128], F32),
+    "E8": ("sbuf", [128, 128], BF), "Z8": ("sbuf", [128, 144], BF),
+    "IB": ("sbuf", [128, 128], BF), "I64": ("sbuf", [128, 128], BF), "I2": ("sbuf", [128, 128], BF), "IN": ("sbuf", [128, 128], BF),
+    "IQ": ("sbuf", [128, 128], F32), "IP": ("sbuf", [128, 128], F32),
+    "QR": ("sbuf", [128, 128], F32), "RT": ("sbuf", [128, 64], F32),
+    "RW": ("sbuf", [128, 12, 2, 32], BF),
+    "PC": ("sbuf", [128, 3, 64], BF), "WW": ("sbuf", [128, 64], F32), "R1": ("sbuf", [128, 64], F32),
+    "MK": ("sbuf", [128, 192], F32), "SCN": ("sbuf", [128, 14, 192], F32),
+    "EA": ("sbuf", [128, 3, 64], F32), "EB": ("sbuf", [128, 3, 64], F32),
+    "SS": ("sbuf", [128, 2, 64], F32), "YA": ("sbuf", [128, 64], F32),
+    "YT": ("sbuf", [128, 64], F32), "YB": ("sbuf", [128, 128], F32),
+}
+for _o in range(3):
+    SCRATCH["MS%d" % _o] = ("sbuf", [128, 4, 64], F32)
+    SCRATCH["LD%d" % _o] = ("sbuf", [128, 4, 64], F32)
+for _b in range(8):
+    SCRATCH["P%d" % _b] = ("psum", [128, 512], F32)
+SEMAPHORES = ["qv", "qs", "qt", "qg", "dC", "dQ", "dG", "dY", "sent", "crd1", "crd2",
+              "a00", "a01", "a10", "a11", "a2", "e0", "e10", "e11", "e2"]
+
+
+def bits(es):
+    return sum(1 << e for e in es)
+
+
+def rank_program(g, core, T, topo):
+    rank = T.rank_of(core)
+    if rank is None:
+        return
+    A = AluOpType
+    COPY, ABS = ActivationFunctionType.Copy, ActivationFunctionType.Abs
+    qs = {"v": g.vector, "s": g.scalar, "t": g.tensor, "g": g, "y": g.sync}
+    sem = {"v": T.sem.qv, "s": T.sem.qs, "t": T.sem.qt, "g": T.sem.qg}
+    cnt = {"v": 0, "s": 0, "t": 0, "g": 0}
+    known = {q: {"v": 0, "s": 0, "t": 0, "g": 0} for q in qs}
+    sent = [0]
+
+    def need(q, *toks):
+        top = {}
+        for tk in toks:
+            top[tk[0]] = max(top.get(tk[0], 0), tk[1])
+        for p, n in top.items():
+            if known[q][p] < n:
+                qs[q].wait_ge(sem[p], n)
+                known[q][p] = n
+
+    def did(q, inst):
+        inst.then_inc(sem[q], 1)
+        cnt[q] += 1
+        return (q, cnt[q])
+
+    V, S = g.vector, g.scalar
+
+    def vcopy(out, in_, *toks):
+        need("v", *toks)
+        return did("v", V.tensor_copy(out, in_))
+
+    def vtt(out, a, b, op, *toks):
+        need("v", *toks)
+        return did("v", V.tensor_tensor(out, a, b, op))
+
+    def act(out, in_, *toks):
+        need("s", *toks)
+        return did("s", S.activation(out, in_, COPY))
+
+    def mm(out, lhsT, rhs, start, stop, *toks):
+        need("t", *toks)
+        return did("t", g.tensor.matmul(out, lhsT, rhs, start, stop))
+
+    def select(out, in_, pattern, op, base, cm, *toks):
+        need("g", *toks)
+        return did("g", g.affine_select(out, in_, pattern, op, 0.0, base, cm))
+
+    def gcopy(counts):
+        return lambda out, in_, *toks: select(out, in_, [[0, n] for n in counts], A.is_ge, 0, 0, ("g", cnt["g"]), *toks)
+
+    P = [T["P%d" % b] for b in range(8)]
+    peer = {k: T.cores[(rank + k) % NR] for k in range(1, NR)}
+    MS = [T["MS%d" % o] for o in range(3)]
+    LD = [T["LD%d" % o] for o in range(3)]
+    CC = [slice(0, 32), slice(32, 64)]
+    ALL = slice(0, 64)
+    late = [[T.sem["a%d%d" % (o, c)] for c in range(2)] for o in range(2)]
+    early = [T.sem.e10, T.sem.e11]
+    full = topo.engines(core, peer[1])
+    h0, h1 = full[:len(full) // 2], full[len(full) // 2:]
+
+    def send(parts, *toks):
+        need("g", *toks)
+        tr = []
+        for k, dst, src, rs, es in parts:
+            rid, pid, _ = topo.addr(peer[k])
+            tr.append(RemoteDMATransfer(dst_ids=[DstId(rid=rid, pnc=pid)], dma_engine_mask=bits(es), remote_sem=rs, src=src, dst=dst))
+            sent[0] += len(es)
+        g.remote_dma_fused(tr, local_sem=T.sem.sent)
+
+    g.sync.dma_start(T.C8i[0:8, 0:64], T.px[:, :]).then_inc(T.sem.dC, 16)
+    g.scalar.dma_start(T.C8i[0:8, 64:128], T.py[:, :]).then_inc(T.sem.dC, 16)
+    g.sync.dma_start(T.Gt[:, :], T.green[:, :]).then_inc(T.sem.dG, 16)
+    g.scalar.dma_start(T.QR[:, 0:64], T.q[:, :]).then_inc(T.sem.dQ, 16)
+    g.scalar.dma_start(T.QR[:, 64:128], T.refl[:, :]).then_inc(T.sem.dQ, 16)
+
+    onb = did("v", V.memset(T.ONB[:, :], 1.0))
+    onf = did("v", V.memset(T.ONF[:, :], 1.0))
+    rz = did("v", V.memset(T.RW[:, :, :, :], 0.0))
+    mk = did("v", V.memset(T.MK[:, :], 1.0))
+    need("v", mk)
+    did("v", V.memset(T.MK[:, 0:192:3], 0.0))
+    e8 = select(T.E8[0:8, :], T.ONB[0:8, 0:128], [[1, 128]], A.is_ge, 0, -16, onb)
+    e8 = select(T.E8[0:8, :], T.E8[0:8, :], [[-1, 128]], A.is_ge, 15, 16, e8)
+    z8 = select(T.Z8[0:8, :], T.ONB[0:8, :], [[1, 144]], A.is_equal, -15, -16)
+    ib = select(T.IB[:, :], T.ONB[:, 0:128], [[-1, 128]], A.is_equal, 0, 1)
+    for ah in range(2):
+        iq = select(T.IQ[:, 64 * ah:64 * ah + 64], T.ONF[:, 0:64], [[-16, 2], [-1, 16], [-32, 2]], A.is_equal, -64 * ah, 1, onf)
+
+    V.wait_ge(T.sem.dC, 32)
+    c8 = vcopy(T.C8b[0:8, :], T.C8i[0:8, :])
+    bc = mm(P[4][:, 0:128], T.E8[0:8, :], T.C8b[0:8, :], True, True, e8, c8)
+    for a in range(16):
+        bs = mm(P[5][:, 0:8], T.Z8[0:8, 15 - a:143 - a], T.C8b[0:8, a:128:16], a == 0, a == 15, z8)
+    clt = vcopy(T.CLT[:, 0, :], P[4][:, 0:128], bc)
+    sc = vcopy(T.SCf[:, 0:8], P[5][:, 0:8], bs)
+    scy = did("v", V.tensor_scalar(T.SCf[:, 8:12], P[5][:, 4:8], 0.5, None, A.mult))
+    send([(3, T.CLT[:, 1, :], T.CLT[:, 0, :], T.sem.crd1, full)], clt)
+    send([(2, T.CLT[:, 2, :], T.CLT[:, 0, :], T.sem.crd2, h0), (1, T.CLT[:, 3, :], T.CLT[:, 0, :], T.sem.crd2, h1)])
+
+    def offs_s(ks, *toks):
+        need("s", *toks)
+        for jj in range(4):
+            t = did("s", S.activation(T.DX[:, ks, :, jj], T.CLT[:, ks, 0:64], ABS, bias=T.SCf[:, jj:jj + 1], scale=-1.0))
+        return t
+
+    def offs_v(ks, *toks):
+        need("v", *toks)
+        for jj in range(4):
+            t = did("v", V.tensor_scalar(T.RA[:, ks, :, jj], T.CLT[:, ks, 64:128], T.SCf[:, 4 + jj:5 + jj], T.SCf[:, 8 + jj:9 + jj], A.max, A.subtract))
+        return t
+
+    def offs_t(k, ps, base, *toks):
+        need("t", *toks)
+        for jj in range(4):
+            out = ps[:, base + jj:base + 256:4]
+            mm(out, T.I64[:, :], T.DX[:, k, :, jj], True, False)
+            mm(out, T.I2[:, :], T.RA[:, k, :, jj], False, False)
+            t = mm(out, T.IN[:, :], T.CLT[:, k, 64:128], False, True)
+        return t
+
+    ox = offs_s(0, clt, sc)
+    oy = offs_v(0, clt, sc, scy)
+    need("v", ib)
+    did("v", V.tensor_scalar(T.I64[:, :], T.IB[:, :], 64.0, None, A.mult))
+    did("v", V.tensor_scalar(T.I2[:, :], T.IB[:, :], 2.0, None, A.mult))
+    idn = did("v", V.tensor_scalar(T.IN[:, :], T.IB[:, :], -1.0, None, A.mult))
+    ot = offs_t(0, P[6], 0, ox, oy, idn)
+    off0 = vcopy(T.OFF[:, 0:256], P[6][:, 0:256], ot)
+
+    def pieces(cols, hi, copiers):
+        r1, w = T.R1[:, cols], T.WW[:, cols]
+        need("v", hi)
+        m = did("v", V.tensor_tensor(T.PC[:, 1, cols], w, T.PC[:, 0, cols], A.subtract))
+        r = did("v", V.tensor_tensor(r1, w, T.PC[:, 0, cols], A.subtract))
+        lo = vtt(T.PC[:, 2, cols], r1, T.PC[:, 1, cols], A.subtract, m, r)
+        last = []
+        for a in range(4):
+            for jh in range(2):
+                ah, a2 = divmod(a, 2)
+                n0, p0 = 6 * a2 + 3 * ah, 64 * ah + 32 * jh
+                src = T.PC[p0:p0 + 32, :, cols.start + a2:cols.stop:2]
+                dst = T.RW[32 * a:32 * a + 32, n0:n0 + 3, jh, cols.start // 2:cols.stop // 2]
+                last.append(copiers[a2](dst, src, lo))
+        return last
+
+    g.tensor.wait_ge(T.sem.dQ, 32)
+    qt = mm(P[3][:, 0:128], T.QR[:, :], T.IQ[:, :], True, True, iq)
+    for ah in range(2):
+        qe = vcopy(T.WW[64 * ah:64 * ah + 64, :], P[3][0:64, ah * 64:ah * 64 + 64], qt)
+    hi = vcopy(T.PC[:, 0, :], T.WW[:, :], qe)
+    rw = pieces(ALL, hi, [gcopy([3, 32])] * 2) + [rz]
+    for ah in range(2):
+        vcopy(T.RT[64 * ah:64 * ah + 64, :], P[3][64:128, ah * 64:ah * 64 + 64])
+    ip = select(T.IP[:, :], T.ONF[:, :], [[-64, 2], [-1, 64]], A.is_equal, 0, 1, *rw)
+
+    def gather(q, k, u0, u1, *toks):
+        a, b = k * 4096 + u0 * 512, k * 4096 + u1 * 512
+        return (act if q == "s" else vcopy)(T.Mg[:, a:b], T.Gt[:, 0:4096].indirect(T.OFF[:, a // 16:b // 16]), *toks)
+
+    def turn(k, u0, u1, *toks):
+        a, b = k * 4096 + u0 * 512, k * 4096 + u1 * 512
+        need("v", *toks)
+        if k == 0:
+            lo = 65 * 8 * u0
+            z = did("v", V.memset(T.Mg[:, lo:min(lo + 65 * 8 * (u1 - u0), 4096):65], 0.0))
+            need("v", z)
+        return did("v", V.transpose(T.Tt[:, a:b], T.Mg[:, a:b]))
+
+    def field(c, t0, nt, ps, p0, *toks, xs=range(16)):
+        need("t", *toks)
+        for x in xs:
+            for jh in range(2):
+                o = jh * 32 + 16 * c + x
+                t = mm(ps[p0:p0 + nt, 12 * x:12 * x + 12], T.Tt[:, t0 * 64 + o:(t0 + nt) * 64:64], T.RW[:, :, jh, 16 * c + x], jh == 0, jh == 1)
+        return t
+
+    def block(k, b, toks):
+        bank, p0 = ((4, 0), (0, 0), (0, 64), (2, 0))[k]
+        return [field(c, 64 * k + 32 * b, 32, P[bank + c], p0 + 32 * b, *toks, *rw) for c in range(2)]
+
+    nac = [0]
+
+    def scan(np_, *banks):
+        i = nac[0]
+        nac[0] += 1
+        for ps, a, b, tok in banks:
+            need("v", tok)
+            t = did("v", V.tensor_tensor_scan(T.SCN[0:np_, i, a:b], T.MK[0:np_, a:b], ps[0:np_, a:b], 0.0, A.mult, A.add))
+        return i, t
+
+    def part(i, h, ah):
+        return T.SCN[64 * h:64 * h + 64, i, 3 * ah + 2:192:6]
+
+    copier = {"v": vcopy, "s": act, "g": gcopy([32])}
+
+    def evac(o, c, banks, slots):
+        i, t = scan(64 * len(slots), *banks)
+        res = {}
+        for h, k, who in slots:
+            res[k] = [copier[who[ah]]((LD if k == 0 else MS)[o][64 * ah:64 * ah + 64, k, CC[c]], part(i, h, ah), t) for ah in range(2)]
+        return res
+
+    def msg(o, cs, k, rs, es):
+        return (k, LD[o][:, k, cs], MS[o][:, k, cs], rs, es)
+
+    made, turned, tok, done, e12 = {}, {}, {("off", 0): off0}, {}, []
+    crd = {1: T.sem.crd1, 2: T.sem.crd2}
+
+    def share(q, plan):
+        for what, k, u0, u1 in plan:
+            if what == "gather":
+                t = gather(q, k, u0, u1, tok["off", k])
+                made.update({(k, u): t for u in range(u0, u1)})
+            elif what == "turn":
+                while any((k, u) not in made for u in range(u0, u1)):
+                    next(scalar)
+                t = turn(k, u0, u1, *[made[k, u] for u in range(u0, u1)])
+                turned.update({(k, u): t for u in range(u0, u1)})
+                for b in range(u0 // 4, (u1 + 3) // 4):
+                    toks = [turned[k, u] for u in range(4 * b, 4 * b + 4) if (k, u) in turned]
+                    if len(toks) == 4:
+                        done[k] = block(k, b, toks)
+            elif what == "places":
+                qs[q].wait_ge(crd[k], len(full))
+                tok[q, k] = (offs_s if q == "s" else offs_v)(slice(u0, u1))
+            elif what == "offsets":
+                while ("s", k) not in tok:
+                    next(scalar)
+                for i in range(u0, u1):
+                    tok["t", k] = offs_t(i, P[5 + k], 256 * (i - u0), tok["s", k], tok["v", k], off0)
+            elif what == "list":
+                t = vcopy(T.OFF[:, 256 * u0:256 * u1], P[5 + k][:, 0:256 * (u1 - u0)], tok["t", k])
+                tok.update({("off", i): t for i in range(u0, u1)})
+            elif k == 3:
+                c = u0
+                e = evac(0, c, [(P[2 + c], 0, 192, done[3][c])], [(0, 3, COPIERS["3"])])
+                send([msg(0, CC[c], 3, late[0][c], full)], *e[3])
+            else:
+                c = u0
+                e = evac(0, c, [(P[c], 0, 192, max(done[1][c], done[2][c]))], [(0, 1, COPIERS["12"][0]), (1, 2, COPIERS["12"][1])])
+                e12.extend(e[1] + e[2])
+                if len(e12) == 8:
+                    send([msg(0, ALL, 1, T.sem.e0, h0), msg(0, ALL, 2, T.sem.e0, h1)], *e12)
+            yield what
+
+    S.wait_ge(T.sem.dG, 16)
+    V.wait_ge(T.sem.dG, 16)
+    scalar = share("s", SPLAN)
+    for _ in share("v", VPLAN):
+        pass
+    for _ in scalar:
+        pass
+
+    mine = {}
+
+    def early_sum(o, c):
+        if o == 0:
+            i, t = scan(64, (P[4 + c], 0, 192, done[0][c]))
+            if c == 0:
+                V.wait_ge(T.sem.e0, len(full))
+                need("v", vtt(T.EA[:, 0, :], LD[0][:, 1, :], LD[0][:, 2, :], A.add))
+            need("v", t)
+            for ah in range(2):
+                r = slice(64 * ah, 64 * ah + 64)
+                e = did("v", V.tensor_tensor(T.EB[r, 0, CC[c]], T.EA[r, 0, CC[c]], part(i, 0, ah), A.add))
+            return e
+        V.wait_ge(early[c], len(full))
+        t = vtt(T.EA[:, 1, CC[c]], LD[1][:, 2, CC[c]], LD[1][:, 3, CC[c]], A.add)
+        return vtt(T.EB[:, 1, CC[c]], T.EA[:, 1, CC[c]], LD[1][:, 0, CC[c]], A.add, t, *mine[c])
+
+    banks = {1: [(6, 7, 0), (1, 2, 3)], 2: [(4, 5, 6), (7, 0, 1)]}
+    e0 = [early_sum(0, c) for c in range(2)]
+    for o in (1, 2):
+        f = []
+        for c in range(2):
+            e = e0[c] if o == 1 else early_sum(1, c)
+            V.wait_ge(late[o - 1][c], len(full))
+            s = vtt(T.SS[:, o - 1, CC[c]], T.EB[:, o - 1, CC[c]], LD[o - 1][:, 3 if o == 1 else 1, CC[c]], A.add, e)
+            need("v", s)
+            did("v", V.tensor_tensor(T.PC[:, 0, CC[c]], T.SS[:, o - 1, CC[c]], T.RT[:, CC[c]], A.mult))
+            hi = did("v", V.tensor_tensor(T.WW[:, CC[c]], T.SS[:, o - 1, CC[c]], T.RT[:, CC[c]], A.mult))
+            r = pieces(CC[c], hi, [vcopy, act])
+            bk = [P[b] for b in banks[o][c]]
+            fb = field(c, 128, 128, bk[0], 0, *r)
+            fa = [field(c, 0, 128, bk[1 + i], 0, xs=range(8 * i, 8 * i + 8)) for i in range(2)]
+            f.append(([(bk[0], 0, 192, fb)], [(bk[1 + i], 96 * i, 96 * i + 96, fa[i]) for i in range(2)]))
+
+        def first(c):
+            return evac(o, c, f[c][0], [(0, 2, COPIERS["fb"][0]), (1, 3, COPIERS["fb"][1])])
+
+        def second(c):
+            return evac(o, c, f[c][1], [(1, 1, COPIERS["fa"][0]), (0, 0, COPIERS["fa"][1])])
+
+        if o == 1:
+            for c in range(2):
+                e = first(c)
+                send([msg(o, CC[c], 2, early[c], h0), msg(o, CC[c], 3, early[c], h1)], *e[2], *e[3])
+                e = second(c)
+                send([msg(o, CC[c], 1, late[o][c], full)], *e[1])
+                mine[c] = e[0]
+        else:
+            ya = vtt(T.YA[:, :], T.SS[:, 0, :], T.SS[:, 1, :], A.add)
+            e = [first(c) for c in range(2)]
+            send([msg(o, ALL, 2, T.sem.e2, h0), msg(o, ALL, 3, T.sem.e2, h1)], *e[0][2], *e[0][3], *e[1][2], *e[1][3])
+            e = [second(c) for c in range(2)]
+            send([msg(o, ALL, 1, T.sem.a2, full)], *e[0][1], *e[1][1])
+            own = vtt(LD[o][:, 0, :], LD[o][:, 0, :], T.YA[:, :], A.add, ya, *e[0][0], *e[1][0])
+
+    V.wait_ge(T.sem.e2, len(full))
+    t = vtt(T.EA[:, 2, :], LD[2][:, 2, :], LD[2][:, 3, :], A.add)
+    e = vtt(T.EB[:, 2, :], T.EA[:, 2, :], LD[2][:, 0, :], A.add, t, own)
+    V.wait_ge(T.sem.a2, len(full))
+    for a2 in range(2):
+        y = vtt(T.YT[:, 32 * a2:32 * a2 + 32], T.EB[:, 2, a2:64:2], LD[2][:, 1, a2:64:2], A.add, e)
+    yt = mm(P[7][0:64, 256:384], T.YT[:, :], T.IP[:, :], True, True, y, ip)
+    yb = vcopy(T.YB[0:64, :], P[7][0:64, 256:384], yt)
+    need("y", yb)
+    g.sync.dma_start(T.y[0:64, :], T.YB[0:64, 0:64]).then_inc(T.sem.dY, 16)
+    need("s", yb)
+    g.scalar.dma_start(T.y[64:128, :], T.YB[0:64, 64:128]).then_inc(T.sem.dY, 16)
+    g.sync.wait_ge(T.sem.dY, 32)
+    need("g", *[(q, cnt[q]) for q in cnt])
+    g.wait_ge(T.sem.sent, sent[0])

@@ -3,50 +3,63 @@ from concourse.mybir import AluOpType, ActivationFunctionType
 
 NR = 4
 F32, BF = "float32", "bfloat16"
-SPLAN = [("gather", 0, 0, 2), ("gather", 0, 2, 3), ("places", 1, 1, 2), ("places", 2, 2, 4), ("gather", 1, 2, 6), ("gather", 2, 0, 5),
-         ("gather", 3, 3, 8), ("gather", 3, 0, 3), ("gather", 0, 5, 8)]
-VPLAN = [("gather", 0, 3, 5), ("places", 1, 1, 2), ("turn", 0, 0, 3), ("offsets", 1, 1, 2), ("list", 1, 1, 2), ("places", 2, 2, 4),
-         ("offsets", 2, 2, 4), ("gather", 1, 0, 2), ("list", 2, 2, 4), ("gather", 1, 6, 8), ("turn", 0, 3, 5), ("turn", 1, 0, 8),
-         ("gather", 2, 5, 8), ("turn", 2, 0, 5), ("turn", 2, 5, 8), ("turn", 3, 4, 8), ("evac", 1, 0, 0), ("evac", 1, 1, 0),
-         ("turn", 3, 0, 4), ("evac", 3, 0, 0), ("turn", 0, 5, 8), ("evac", 3, 1, 0)]
-COPIERS = {"12": ["gv", "gv"], "3": "vv", "fb": ["vs", "vs"], "fa": ["vs", "vs"]}
+W = 4096 + 16
+TILES = [((0, 0), (0, 1)), ((2, 0), (2, 1)), ((1, 0), (3, 0)), ((1, 1), (3, 1))]
+SPLAN = [("dist", 1), ("gather", 0, 0, 2), ("dist", 2), ("gather", 0, 2, 4), ("dist", 3), ("gather", 1, 0, 6), ("gather", 2, 0, 4),
+         ("gather", 2, 4, 6), ("gather", 3, 0, 4), ("gather", 3, 4, 7)]
+VPLAN = [("gather", 0, 7, 8), ("list", 1), ("turn q",), ("gather", 0, 4, 7), ("list", 2), ("q",), ("turn", 0, 0, 8), ("list", 3),
+         ("gather", 1, 6, 8), ("turn", 1, 0, 8), ("gather", 2, 6, 8), ("turn", 2, 0, 4), ("turn", 2, 4, 8), ("gather", 3, 7, 8),
+         ("order", 0, 0, 0), ("run", 0, 1, 0, 0, 16), ("turn", 3, 0, 4), ("order", 0, 1, 0), ("turn", 3, 4, 8), ("run", 0, 2, 0, 0, 8)]
+TAIL = [("order", 1, 0, 0), ("run", 1, 1, 0, 0, 8), ("order", 1, 0, 1), ("run", 1, 1, 1, 8, 16), ("run", 0, 2, 0, 8, 16),
+        ("order", 1, 1, 0), ("run", 1, 2, 0, 0, 8), ("order", 1, 1, 1), ("run", 1, 2, 1, 8, 16),
+        ("order", 0, 2, 0), ("order", 1, 2, 0), ("order", 1, 2, 1)]
 SCRATCH = {
-    "Gt": ("sbuf", [128, 4096], BF),
-    "Mg": ("sbuf", [128, 16384], BF),
-    "Tt": ("sbuf", [128, 16384], BF),
-    "OFF": ("sbuf", [128, 1024], "uint16"),
-    "DX": ("sbuf", [128, 4, 64, 4], BF), "RA": ("sbuf", [128, 4, 64, 4], BF),
-    "C8i": ("sbuf", [128, 128], "int32"), "C8b": ("sbuf", [128, 128], BF),
-    "SCf": ("sbuf", [128, 12], F32),
-    "CLT": ("sbuf", [128, 4, 128], BF),
-    "ONB": ("sbuf", [128, 144], BF), "ONF": ("sbuf", [128, 128], F32),
-    "E8": ("sbuf", [128, 128], BF), "Z8": ("sbuf", [128, 144], BF),
-    "IB": ("sbuf", [128, 128], BF), "I64": ("sbuf", [128, 128], BF), "I2": ("sbuf", [128, 128], BF), "IN": ("sbuf", [128, 128], BF),
-    "IQ": ("sbuf", [128, 128], F32), "IP": ("sbuf", [128, 128], F32),
-    "QR": ("sbuf", [128, 128], F32), "RT": ("sbuf", [128, 64], F32),
-    "RW": ("sbuf", [128, 12, 2, 32], BF),
-    "PC": ("sbuf", [128, 3, 64], BF), "WW": ("sbuf", [128, 64], F32), "R1": ("sbuf", [128, 64], F32),
-    "MK": ("sbuf", [128, 192], F32), "SCN": ("sbuf", [128, 14, 192], F32),
-    "EA": ("sbuf", [128, 3, 64], F32), "EB": ("sbuf", [128, 3, 64], F32),
-    "SS": ("sbuf", [128, 2, 64], F32), "YA": ("sbuf", [128, 64], F32),
-    "YT": ("sbuf", [128, 64], F32), "YB": ("sbuf", [128, 128], F32),
+    "SP": ("dram", [4, 128, 2], "int32"), "RP": ("dram", [4, 128, 2], "int32"),
+    "SQ": ("dram", [4, 128, 32], F32), "RQ": ("dram", [4, 128, 32], F32),
+    "SC": ("dram", [128, 1024], BF), "RC": ("dram", [128, 1024], BF),
+    "SB": ("dram", [2, 128, 512], BF), "RB": ("dram", [2, 128, 512], BF),
+    "SA": ("dram", [2, 128, 512], BF), "RA": ("dram", [2, 128, 512], BF),
+    "Gt": ("sbuf", [128, 4 * W], BF), "Mg": ("sbuf", [128, 16384], BF), "Tt": ("sbuf", [128, 16384], BF),
+    "OFF": ("sbuf", [128, 1024], "uint16"), "DD": ("sbuf", [128, 16, 128], BF),
+    "PLi": ("sbuf", [128, 128], "int32"), "PL": ("sbuf", [128, 128], BF),
+    "PT": ("sbuf", [128, 16], BF), "S0": ("sbuf", [128, 4], F32), "S1": ("sbuf", [128, 12], F32),
+    "ONF": ("sbuf", [128, 128], F32), "IF": ("sbuf", [128, 128], F32), "IQ": ("sbuf", [128, 128], F32),
+    "IB": ("sbuf", [128, 8, 16], BF), "I64": ("sbuf", [128, 128], BF), "IK": ("sbuf", [128, 128], BF),
+    "E": ("sbuf", [128, 6, 4, 32], BF), "PM": ("sbuf", [128, 4, 2, 32], BF), "ZB": ("sbuf", [128, 256], BF),
+    "QN": ("sbuf", [128, 128], F32), "WQ": ("sbuf", [128, 64], F32),
+    "PC": ("sbuf", [128, 3, 64], BF), "R1": ("sbuf", [128, 64], F32), "RW": ("sbuf", [128, 2, 8, 64], BF),
+    "MK": ("sbuf", [128, 256], F32), "SCN": ("sbuf", [128, 6, 128], F32), "YA": ("sbuf", [128, 64], F32),
+    "YS": ("sbuf", [128, 64], F32), "YB": ("sbuf", [128, 64], F32), "LY": ("sbuf", [128, 4, 64], F32),
 }
-for _o in range(3):
-    SCRATCH["MS%d" % _o] = ("sbuf", [128, 4, 64], F32)
-    SCRATCH["LD%d" % _o] = ("sbuf", [128, 4, 64], F32)
 for _b in range(8):
     SCRATCH["P%d" % _b] = ("psum", [128, 512], F32)
-SEMAPHORES = ["qv", "qs", "qt", "qg", "dC", "dQ", "dG", "dY", "sent", "crd1", "crd2",
-              "a00", "a01", "a10", "a11", "a2", "e0", "e10", "e11", "e2"]
+SEMAPHORES = ["qv", "qs", "qt", "qg", "dP", "dO", "dQ", "dC", "dA", "dL", "dN", "dG0", "dG1", "dG2", "dG3", "dY", "sent",
+              "aP", "aQ", "aC", "aA", "aB", "dB", "aY"]
 
 
 def bits(es):
     return sum(1 << e for e in es)
 
 
+def helpers(topo, core):
+    far = [c for c in topo.cores_of(core) if topo.die(c) != topo.die(core)]
+    return [far[0], [c for c in far if topo.addr(c)[2] != topo.addr(far[0])[2]][0]]
+
+
+def helper_program(g, core, T, topo, rank, n):
+    to = T.cores[(rank + (3, 1)[n]) % NR]
+    rid, pid, _ = topo.addr(to)
+    g.wait_ge(T.sem.aA, (len(topo.engines(T.cores[rank], core)) - len(topo.engines(T.cores[rank], to))) // 2)
+    g.remote_dma(T.RA[n], T.SA[n], T.sem.aA, T.sem.sent, pid, rid, topo.mask(core, to))
+    g.wait_ge(T.sem.sent, len(topo.engines(core, to)))
+
+
 def rank_program(g, core, T, topo):
     rank = T.rank_of(core)
     if rank is None:
+        for r, boss in enumerate(T.cores):
+            if core in helpers(topo, boss):
+                helper_program(g, core, T, topo, r, helpers(topo, boss).index(core))
         return
     A = AluOpType
     COPY, ABS = ActivationFunctionType.Copy, ActivationFunctionType.Abs
@@ -55,6 +68,7 @@ def rank_program(g, core, T, topo):
     cnt = {"v": 0, "s": 0, "t": 0, "g": 0}
     known = {q: {"v": 0, "s": 0, "t": 0, "g": 0} for q in qs}
     sent = [0]
+    V, S, Y = g.vector, g.scalar, g.sync
 
     def need(q, *toks):
         top = {}
@@ -70,7 +84,8 @@ def rank_program(g, core, T, topo):
         cnt[q] += 1
         return (q, cnt[q])
 
-    V, S = g.vector, g.scalar
+    def fill(ap, value):
+        return did("v", V.memset(ap, value))
 
     def vcopy(out, in_, *toks):
         need("v", *toks)
@@ -80,292 +95,296 @@ def rank_program(g, core, T, topo):
         need("v", *toks)
         return did("v", V.tensor_tensor(out, a, b, op))
 
-    def act(out, in_, *toks):
+    def act(out, in_, *toks, scale=1.0):
         need("s", *toks)
-        return did("s", S.activation(out, in_, COPY))
+        return did("s", S.activation(out, in_, COPY, scale=scale))
 
     def mm(out, lhsT, rhs, start, stop, *toks):
         need("t", *toks)
         return did("t", g.tensor.matmul(out, lhsT, rhs, start, stop))
 
-    def select(out, in_, pattern, op, base, cm, *toks):
+    def select(out, in_, pattern, op, cm, *toks):
         need("g", *toks)
-        return did("g", g.affine_select(out, in_, pattern, op, 0.0, base, cm))
+        return did("g", g.affine_select(out, in_, pattern, op, 0.0, 0, cm))
 
-    def gcopy(counts):
-        return lambda out, in_, *toks: select(out, in_, [[0, n] for n in counts], A.is_ge, 0, 0, ("g", cnt["g"]), *toks)
+    def gcopy(n):
+        return lambda out, in_, *toks: select(out, in_, [[0, 3], [0, n]], A.is_ge, 0, ("g", cnt["g"]), *toks)
+
+    def dma(q, out, in_, s):
+        q.dma_start(out, in_).then_inc(s, 16)
 
     P = [T["P%d" % b] for b in range(8)]
-    peer = {k: T.cores[(rank + k) % NR] for k in range(1, NR)}
-    MS = [T["MS%d" % o] for o in range(3)]
-    LD = [T["LD%d" % o] for o in range(3)]
-    CC = [slice(0, 32), slice(32, 64)]
-    ALL = slice(0, 64)
-    late = [[T.sem["a%d%d" % (o, c)] for c in range(2)] for o in range(2)]
-    early = [T.sem.e10, T.sem.e11]
-    full = topo.engines(core, peer[1])
-    h0, h1 = full[:len(full) // 2], full[len(full) // 2:]
+    who = [(rank + k) % NR for k in range(NR)]
+    full = topo.engines(core, T.cores[who[1]])
+    quarter = len(full) // 4
+    peer = [T.cores[r] for r in who]
 
-    def send(parts, *toks):
-        need("g", *toks)
+    def send(parts):
         tr = []
-        for k, dst, src, rs, es in parts:
-            rid, pid, _ = topo.addr(peer[k])
-            tr.append(RemoteDMATransfer(dst_ids=[DstId(rid=rid, pnc=pid)], dma_engine_mask=bits(es), remote_sem=rs, src=src, dst=dst))
+        for cs, dsts, src, rs, es in parts:
+            ids = [DstId(rid=topo.addr(c)[0], pnc=topo.addr(c)[1]) for c in cs]
+            tr.append(RemoteDMATransfer(dst_ids=ids, dma_engine_mask=bits(es), remote_sem=rs, srcs=[src], dsts=dsts))
             sent[0] += len(es)
         g.remote_dma_fused(tr, local_sem=T.sem.sent)
 
-    g.sync.dma_start(T.C8i[0:8, 0:64], T.px[:, :]).then_inc(T.sem.dC, 16)
-    g.scalar.dma_start(T.C8i[0:8, 64:128], T.py[:, :]).then_inc(T.sem.dC, 16)
-    g.sync.dma_start(T.Gt[:, :], T.green[:, :]).then_inc(T.sem.dG, 16)
-    g.scalar.dma_start(T.QR[:, 0:64], T.q[:, :]).then_inc(T.sem.dQ, 16)
-    g.scalar.dma_start(T.QR[:, 64:128], T.refl[:, :]).then_inc(T.sem.dQ, 16)
+    def rows(k, n=32):
+        return slice(n * k, n * k + n)
 
-    onb = did("v", V.memset(T.ONB[:, :], 1.0))
-    onf = did("v", V.memset(T.ONF[:, :], 1.0))
-    rz = did("v", V.memset(T.RW[:, :, :, :], 0.0))
-    mk = did("v", V.memset(T.MK[:, :], 1.0))
+    def table(tile, src, us=range(4)):
+        for u in us:
+            dma(Y, T.Gt[rows(u), W * tile:W * tile + 4096], src, T.sem["dG%d" % tile])
+
+    dma(Y, T.SP[:, 0:64, :], T.px[:, :], T.sem.dP)
+    dma(S, T.SP[:, 64:128, :], T.py[:, :], T.sem.dP)
+    dma(Y, T.PLi[0:2, 0:64], T.px[rows(rank, 2), :], T.sem.dO)
+    dma(S, T.PLi[0:2, 64:128], T.py[rows(rank, 2), :], T.sem.dO)
+    dma(Y, T.SQ[:, 0:64, :], T.q[:, :], T.sem.dQ)
+    dma(S, T.SQ[:, 64:128, :], T.refl[:, :], T.sem.dQ)
+    dma(Y, T.SC[:, :], T.green[rows(who[2]), :], T.sem.dC)
+    dma(S, T.QN[0:32, 0:64], T.q[rows(rank), :], T.sem.dN)
+    dma(S, T.QN[0:32, 64:128], T.refl[rows(rank), :], T.sem.dN)
+    for n, k in enumerate((3, 1)):
+        dma(Y, T.SA[n], T.green[rows(2 * who[k], 16), :], T.sem.dA)
+    table(0, T.green[rows(rank), :], (0,))
+
+    onf = fill(T.ONF[:, :], 1.0)
+    idf = select(T.IF[:, :], T.ONF[:, :], [[-1, 128]], A.is_equal, 1, onf)
+    pm = fill(T.PM[0:64, :, :, :], 0.0)
+    for t in range(4):
+        gz = fill(T.Gt[:, W * t + 4096:W * t + W], 0.0)
+    zb = fill(T.ZB[:, :], 0.0)
+    mk = fill(T.MK[:, :], 1.0)
+    rz = fill(T.RW[:, :, :, :], 0.0)
     need("v", mk)
-    did("v", V.memset(T.MK[:, 0:192:3], 0.0))
-    e8 = select(T.E8[0:8, :], T.ONB[0:8, 0:128], [[1, 128]], A.is_ge, 0, -16, onb)
-    e8 = select(T.E8[0:8, :], T.E8[0:8, :], [[-1, 128]], A.is_ge, 15, 16, e8)
-    z8 = select(T.Z8[0:8, :], T.ONB[0:8, :], [[1, 144]], A.is_equal, -15, -16)
-    ib = select(T.IB[:, :], T.ONB[:, 0:128], [[-1, 128]], A.is_equal, 0, 1)
-    for ah in range(2):
-        iq = select(T.IQ[:, 64 * ah:64 * ah + 64], T.ONF[:, 0:64], [[-16, 2], [-1, 16], [-32, 2]], A.is_equal, -64 * ah, 1, onf)
+    mk = fill(T.MK[:, 0:256:4], 0.0)
+    ib = vcopy(T.IB[:, :, :], T.IF[:, :], idf)
+    need("v", pm, ib)
+    for jj in range(2):
+        for b in range(2):
+            pm = vcopy(T.PM[0:64, 2 * jj + b, :, rows(b, 16)], T.IB[0:64, jj:4:2, :])
+    for c in range(2):
+        for k in range(4):
+            e = act(T.E[0:8, 2 + 2 * c + k // 2, rows(k % 2, 2), :], T.ONF[0:8, 0:64], idf, scale=T.IF[0:8, 2 * k + c:2 * k + c + 1])
+    for B in range(2):
+        for b in range(2):
+            ee = vcopy(T.E[0:8, B, :, rows(b, 16)], T.E[0:8, 2 + 2 * b + B, :, 0:16], e)
+    act(T.I64[:, :], T.IF[:, :], scale=64.0)
+    ik = act(T.IK[:, :], T.IF[:, :], scale=4096.0)
 
-    V.wait_ge(T.sem.dC, 32)
-    c8 = vcopy(T.C8b[0:8, :], T.C8i[0:8, :])
-    bc = mm(P[4][:, 0:128], T.E8[0:8, :], T.C8b[0:8, :], True, True, e8, c8)
-    for a in range(16):
-        bs = mm(P[5][:, 0:8], T.Z8[0:8, 15 - a:143 - a], T.C8b[0:8, a:128:16], a == 0, a == 15, z8)
-    clt = vcopy(T.CLT[:, 0, :], P[4][:, 0:128], bc)
-    sc = vcopy(T.SCf[:, 0:8], P[5][:, 0:8], bs)
-    scy = did("v", V.tensor_scalar(T.SCf[:, 8:12], P[5][:, 4:8], 0.5, None, A.mult))
-    send([(3, T.CLT[:, 1, :], T.CLT[:, 0, :], T.sem.crd1, full)], clt)
-    send([(2, T.CLT[:, 2, :], T.CLT[:, 0, :], T.sem.crd2, h0), (1, T.CLT[:, 3, :], T.CLT[:, 0, :], T.sem.crd2, h1)])
+    g.wait_ge(T.sem.dP, 32)
+    send([([peer[k]], [T.RP[NR - k]], T.SP[who[k]], T.sem.aP, [full[quarter * k]]) for k in (1, 2, 3)])
+    g.wait_ge(T.sem.dQ, 32)
+    send([([peer[k]], [T.RQ[NR - k]], T.SQ[who[k]], T.sem.aQ, full[quarter * k:quarter * k + quarter]) for k in (1, 2, 3)])
+    g.wait_ge(T.sem.dC, 16)
+    send([([peer[2]], [T.RC[:, :]], T.SC[:, :], T.sem.aC, full)])
+    g.wait_ge(T.sem.dA, 32)
+    near = [e for e in topo.engines(core, helpers(topo, core)[0]) if e not in full]
+    send([([c], [T.SA[n]], T.SA[n], T.sem.aA, near[rows(n, len(near) // 2)]) for n, c in enumerate(helpers(topo, core))])
+    iq = select(T.IQ[:, :], T.ONF[:, :], [[-64, 2], [-1, 32], [-32, 2]], A.is_equal, 1)
+    for q, o in ((Y, 0), (S, 64)):
+        q.wait_ge(T.sem.aP, 3)
+        dma(q, T.PLi[2:8, o:o + 64], T.RP[1:4, o:o + 64, :], T.sem.dL)
+    table(0, T.green[rows(rank), :], (1, 2, 3))
+    for n, k in enumerate((3, 1)):
+        dma(Y, T.SB[n], T.green[rows(2 * who[k] + 1, 16), :], T.sem.dB)
+    Y.wait_ge(T.sem.aQ, 3 * quarter)
+    for o in (0, 64):
+        dma(Y, T.QN[32:128, o:o + 64], T.RQ[1:4, o:o + 64, :], T.sem.dN)
+    g.wait_ge(T.sem.aC, len(full))
+    g.wait_ge(T.sem.dB, 32)
+    send([([peer[k]], [T.RB[n]], T.SB[n], T.sem.aB, full[rows(n, 2 * quarter)]) for n, k in enumerate((3, 1))])
+    for tile, src, a, n in ((1, T.RC[:, :], T.sem.aC, 1), (2, T.RA[0:2], T.sem.aA, 2), (3, T.RB[0:2], T.sem.aB, 1)):
+        Y.wait_ge(a, n * len(full))
+        table(tile, src)
 
-    def offs_s(ks, *toks):
-        need("s", *toks)
-        for jj in range(4):
-            t = did("s", S.activation(T.DX[:, ks, :, jj], T.CLT[:, ks, 0:64], ABS, bias=T.SCf[:, jj:jj + 1], scale=-1.0))
-        return t
+    def sources(k, picks, c0, c1, out, *toks):
+        n = c1 - c0
+        for xy in range(2):
+            for r0, o, step in picks:
+                t = mm(P[4][0:64, o + xy:o + xy + step + 1:step], T.PL[0:k, rows(xy, 64)], T.IB[0:k, 0, r0:r0 + 2], True, True, *toks)
+        need("v", t)
+        for b in range(2):
+            t = did("v", V.tensor_copy(T.PT[0:64, 8 * b + c0:8 * b + c1], P[4][0:64, 8 * b + c0:8 * b + c1]))
+        for L in range(2):
+            for jj in range(2):
+                for b in range(2):
+                    u = mm(P[4][rows(L, 64), 32 + n * jj:32 + n * jj + n], T.PM[0:64, 2 * jj + b, :, :], T.PT[0:64, 8 * b + c0:8 * b + c1],
+                           b == 0, b == 1, t, pm)
+        return vcopy(out, P[4][:, 32:32 + 2 * n], u), u
 
-    def offs_v(ks, *toks):
-        need("v", *toks)
-        for jj in range(4):
-            t = did("v", V.tensor_scalar(T.RA[:, ks, :, jj], T.CLT[:, ks, 64:128], T.SCf[:, 4 + jj:5 + jj], T.SCf[:, 8 + jj:9 + jj], A.max, A.subtract))
-        return t
+    CL = [(P[0][:, 0:128], P[1][:, 0:128]), (P[2][:, 0:128], P[2][:, 128:256]), (P[2][:, 256:384], P[2][:, 384:512])]
+    OB = [P[3], P[5], P[3], P[1]]
+    tok = {}
 
-    def offs_t(k, ps, base, *toks):
-        need("t", *toks)
-        for jj in range(4):
-            out = ps[:, base + jj:base + 256:4]
-            mm(out, T.I64[:, :], T.DX[:, k, :, jj], True, False)
-            mm(out, T.I2[:, :], T.RA[:, k, :, jj], False, False)
-            t = mm(out, T.IN[:, :], T.CLT[:, k, 64:128], False, True)
-        return t
+    def dist(tile):
+        v = max(tile - 1, 0)
+        need("s", tok["spread", v], tok["src", min(tile, 1)])
+        for xy in range(2):
+            for jj in range(2):
+                o = 2 * jj + xy if tile == 0 else 6 * jj + 2 * tile - 2 + xy
+                tok["dist", tile, xy] = did("s", S.activation(T.DD[:, 4 * tile + 2 * xy + jj, :], CL[v][xy], ABS,
+                                                              bias=(T.S1 if tile else T.S0)[:, o:o + 1], scale=-1.0))
 
-    ox = offs_s(0, clt, sc)
-    oy = offs_v(0, clt, sc, scy)
-    need("v", ib)
-    did("v", V.tensor_scalar(T.I64[:, :], T.IB[:, :], 64.0, None, A.mult))
-    did("v", V.tensor_scalar(T.I2[:, :], T.IB[:, :], 2.0, None, A.mult))
-    idn = did("v", V.tensor_scalar(T.IN[:, :], T.IB[:, :], -1.0, None, A.mult))
-    ot = offs_t(0, P[6], 0, ox, oy, idn)
-    off0 = vcopy(T.OFF[:, 0:256], P[6][:, 0:256], ot)
+    def selves(tile):
+        mm(OB[tile][:, 0:256], T.IB[:, :, :], T.ZB[:, :], True, False, ib, ik, zb, tok.get(("list", tile - 2), ik), tok.get(("dist", tile - 2, 1), ik))
+        for jj in range(2):
+            for b, (k, _) in enumerate(TILES[tile]):
+                for h in range(2):
+                    o = 2 * (64 * (k // 2) + 32 * h + 16 * jj) + jj
+                    mm(OB[tile][:, o:o + 31:2], T.IK[:, :], T.IB[:, 4 * (k % 2) + 2 * h + b, :], False, False)
 
-    def pieces(cols, hi, copiers):
-        r1, w = T.R1[:, cols], T.WW[:, cols]
-        need("v", hi)
-        m = did("v", V.tensor_tensor(T.PC[:, 1, cols], w, T.PC[:, 0, cols], A.subtract))
-        r = did("v", V.tensor_tensor(r1, w, T.PC[:, 0, cols], A.subtract))
+    def offsets(tile):
+        if tile:
+            selves(tile)
+        for xy in range(2):
+            for jj in range(2):
+                t = mm(OB[tile][:, jj:256:2], T.IB[:, :, :] if xy else T.I64[:, :], T.DD[:, 4 * tile + 2 * xy + jj, :], False, xy + jj == 2,
+                       tok["dist", tile, xy])
+        tok["sum", tile] = t
+
+    def listed(tile):
+        tok["list", tile] = vcopy(T.OFF[:, rows(tile, 256)], OB[tile][:, 0:256], tok["sum", tile])
+
+    def pieces(w, cols, copiers, *toks):
+        r1 = T.R1[:, cols]
+        hi = vcopy(T.PC[:, 0, cols], w, *toks)
+        m = vtt(T.PC[:, 1, cols], w, T.PC[:, 0, cols], A.subtract, hi)
+        r = vtt(r1, w, T.PC[:, 0, cols], A.subtract)
         lo = vtt(T.PC[:, 2, cols], r1, T.PC[:, 1, cols], A.subtract, m, r)
-        last = []
-        for a in range(4):
-            for jh in range(2):
-                ah, a2 = divmod(a, 2)
-                n0, p0 = 6 * a2 + 3 * ah, 64 * ah + 32 * jh
-                src = T.PC[p0:p0 + 32, :, cols.start + a2:cols.stop:2]
-                dst = T.RW[32 * a:32 * a + 32, n0:n0 + 3, jh, cols.start // 2:cols.stop // 2]
-                last.append(copiers[a2](dst, src, lo))
-        return last
+        return [copiers[L](T.RW[rows(L, 64), B, 4 * L:4 * L + 3, cols], T.PC[rows(B, 64), :, cols], lo, rz) for B in range(2) for L in range(2)]
 
-    g.tensor.wait_ge(T.sem.dQ, 32)
-    qt = mm(P[3][:, 0:128], T.QR[:, :], T.IQ[:, :], True, True, iq)
-    for ah in range(2):
-        qe = vcopy(T.WW[64 * ah:64 * ah + 64, :], P[3][0:64, ah * 64:ah * 64 + 64], qt)
-    hi = vcopy(T.PC[:, 0, :], T.WW[:, :], qe)
-    rw = pieces(ALL, hi, [gcopy([3, 32])] * 2) + [rz]
-    for ah in range(2):
-        vcopy(T.RT[64 * ah:64 * ah + 64, :], P[3][64:128, ah * 64:ah * 64 + 64])
-    ip = select(T.IP[:, :], T.ONF[:, :], [[-64, 2], [-1, 64]], A.is_equal, 0, 1, *rw)
+    V.wait_ge(T.sem.dO, 32)
+    pl = vcopy(T.PL[0:2, :], T.PLi[0:2, :])
+    tok["src", 0], used = sources(2, [(0, 0, 8)], 0, 2, T.S0[:, :], pl, ib)
+    selves(0)
+    V.wait_ge(T.sem.dL, 32)
+    pl = vcopy(T.PL[0:8, :], T.PLi[0:8, :], used)
 
-    def gather(q, k, u0, u1, *toks):
-        a, b = k * 4096 + u0 * 512, k * 4096 + u1 * 512
-        return (act if q == "s" else vcopy)(T.Mg[:, a:b], T.Gt[:, 0:4096].indirect(T.OFF[:, a // 16:b // 16]), *toks)
-
-    def turn(k, u0, u1, *toks):
-        a, b = k * 4096 + u0 * 512, k * 4096 + u1 * 512
-        need("v", *toks)
-        if k == 0:
-            lo = 65 * 8 * u0
-            z = did("v", V.memset(T.Mg[:, lo:min(lo + 65 * 8 * (u1 - u0), 4096):65], 0.0))
-            need("v", z)
-        return did("v", V.transpose(T.Tt[:, a:b], T.Mg[:, a:b]))
-
-    def field(c, t0, nt, ps, p0, *toks, xs=range(16)):
-        need("t", *toks)
-        for x in xs:
-            for jh in range(2):
-                o = jh * 32 + 16 * c + x
-                t = mm(ps[p0:p0 + nt, 12 * x:12 * x + 12], T.Tt[:, t0 * 64 + o:(t0 + nt) * 64:64], T.RW[:, :, jh, 16 * c + x], jh == 0, jh == 1)
+    def spread(v):
+        for xy in range(2):
+            for B in range(2):
+                bank, o = (P[2], 256 * v - 256 + 128 * xy + 64 * B) if v else (P[xy], 64 * B)
+                t = mm(bank[:, o:o + 64], T.E[0:8, 2 * v + B, :, :], T.PL[0:8, rows(xy, 64)], True, True, pl, ee)
         return t
 
-    def block(k, b, toks):
-        bank, p0 = ((4, 0), (0, 0), (0, 64), (2, 0))[k]
-        return [field(c, 64 * k + 32 * b, 32, P[bank + c], p0 + 32 * b, *toks, *rw) for c in range(2)]
+    tok["spread", 0] = spread(0)
+    dist(0)
+    tok["src", 1], used = sources(8, [(4, 2, 8), (2, 4, 2), (6, 12, 2)], 2, 8, T.S1[:, :], pl, tok["src", 0])
+    offsets(0)
+    listed(0)
+    spread(1)
+    tok["spread", 1] = tok["spread", 2] = spread(2)
 
-    nac = [0]
+    def turn_q():
+        g.tensor.wait_ge(T.sem.dN, 64)
+        for i in range(2):
+            for B in range(2):
+                tok["qt"] = mm(P[6][rows(B, 64), rows(i, 64)], T.QN[:, rows(i, 64)], T.IQ[:, rows(B, 64)], True, True, iq)
 
-    def scan(np_, *banks):
-        i = nac[0]
-        nac[0] += 1
-        for ps, a, b, tok in banks:
-            need("v", tok)
-            t = did("v", V.tensor_tensor_scan(T.SCN[0:np_, i, a:b], T.MK[0:np_, a:b], ps[0:np_, a:b], 0.0, A.mult, A.add))
-        return i, t
+    def start():
+        t = vcopy(T.WQ[:, :], P[6][:, 0:64], tok["qt"])
+        tok["mk"] = vcopy(T.MK[:, 3:256:4], P[6][:, 64:128], mk)
+        tok["rw"] = pieces(T.WQ[:, :], slice(0, 64), [gcopy(64)] * 2, t) + [tok["mk"]]
 
-    def part(i, h, ah):
-        return T.SCN[64 * h:64 * h + 64, i, 3 * ah + 2:192:6]
+    CH = [[range(16)], [range(8), range(8, 16)]]
+    BANK = [[[4], [5], [4]], [[6, 7], [0, 1], [2, 3]]]
+    field = {}
 
-    copier = {"v": vcopy, "s": act, "g": gcopy([32])}
+    def term(c, o, i, x, tile, b, t0, t1, first, last):
+        k, xl = TILES[tile][b][0], x - CH[c][i][0]
+        a = 4096 * tile + 16 * b + x
+        return mm(P[BANK[c][o][i]][t0:t1, 8 * xl:8 * xl + 8], T.Tt[:, a + 32 * t0:a + 32 * t1 - 31:32], T.RW[:, k // 2, :, 32 * c + 2 * x + k % 2], first, last)
 
-    def evac(o, c, banks, slots):
-        i, t = scan(64 * len(slots), *banks)
-        res = {}
-        for h, k, who in slots:
-            res[k] = [copier[who[ah]]((LD if k == 0 else MS)[o][64 * ah:64 * ah + 64, k, CC[c]], part(i, h, ah), t) for ah in range(2)]
-        return res
+    def first_order(tile, t0, t1, *toks):
+        need("t", *toks)
+        for c in range(2):
+            for i, xs in enumerate(CH[c]):
+                if ("open", c, i) not in tok:
+                    tok["open", c, i] = mm(P[BANK[c][0][i]][:, 0:8 * len(xs)], T.IB[:, :, :], T.ZB[:, 0:8 * len(xs)], True, False, tok["src", 1])
+                todo = [(x, b) for x in xs for b in range(2) if TILES[tile][b][1] == c]
+                for x, b in todo:
+                    field[c, 0, i] = term(c, 0, i, x, tile, b, t0, t1, False, tile == 2 + c and (x, b) == todo[-1])
 
-    def msg(o, cs, k, rs, es):
-        return (k, LD[o][:, k, cs], MS[o][:, k, cs], rs, es)
+    def later_order(c, o, i, x0, x1):
+        need("t", *tok["w", c, o, i])
+        src = [(tile, b) for tile in range(4) for b in range(2) if TILES[tile][b][1] == c]
+        for x in range(x0, x1):
+            for n, (tile, b) in enumerate(src):
+                field[c, o, i] = term(c, o, i, x, tile, b, 0, 128, n == 0, n == 3)
 
-    made, turned, tok, done, e12 = {}, {}, {("off", 0): off0}, {}, []
-    crd = {1: T.sem.crd1, 2: T.sem.crd2}
+    got, ya = [], {}
+
+    def order(c, o, i, copiers):
+        xs = CH[c][i]
+        a, b = 8 * xs[0], 8 * xs[-1] + 8
+        cols = slice(32 * c + 2 * xs[0], 32 * c + 2 * xs[-1] + 2)
+        need("v", field[c, o, i], tok["mk"])
+        t = did("v", V.tensor_tensor_scan(T.SCN[:, 3 * c + o, a:b], T.MK[:, 128 * c + a:128 * c + b], P[BANK[c][o][i]][:, 0:b - a], 0.0, A.mult, A.add))
+        if o < 2:
+            tok["w", c, o + 1, i] = pieces(T.SCN[:, 3 * c + o, a + 3:b:4], cols, copiers, t)
+        if o == 1:
+            ya[c, i] = vtt(T.YA[:, cols], T.SCN[:, 3 * c, a + 2:b:4], T.SCN[:, 3 * c + 1, a + 2:b:4], A.add)
+        if o == 2:
+            got.append(vtt(T.YS[:, cols], T.SCN[:, 3 * c + o, a + 2:b:4], T.YA[:, cols], A.add, t, ya[c, i]))
+
+    def finish():
+        for B in range(2):
+            t = mm(P[5][rows(B, 64), 128:192], T.YS[:, :], T.IF[:, rows(B, 64)], True, True, *got)
+        t = vcopy(T.YB[:, :], P[5][:, 128:192], t)
+        need("g", t)
+        send([(peer[1:], [T.LY[:, NR - k, :] for k in (1, 2, 3)], T.YB[:, :], T.sem.aY, full)])
+        need("s", t)
+        dma(S, T.y[rows(rank), :], T.YB[0:64:2, :], T.sem.dY)
+        for q in (Y, S):
+            q.wait_ge(T.sem.aY, 3 * len(full))
+        for k in (1, 2, 3):
+            B, L = divmod(NR - k, 2)
+            dma((Y, S)[k == 2], T.y[rows(who[k]), :], T.LY[64 * B + L:64 * B + 64:2, k, :], T.sem.dY)
+
+    made, loaded = {}, set()
 
     def share(q, plan):
-        for what, k, u0, u1 in plan:
+        for what, *arg in plan:
             if what == "gather":
-                t = gather(q, k, u0, u1, tok["off", k])
-                made.update({(k, u): t for u in range(u0, u1)})
+                tile, u0, u1 = arg
+                while ("list", tile) not in tok:
+                    yield False
+                if (q, tile) not in loaded:
+                    qs[q].wait_ge(T.sem["dG%d" % tile], 64)
+                    loaded.add((q, tile))
+                a, b = 4096 * tile + 512 * u0, 4096 * tile + 512 * u1
+                t = (act if q == "s" else vcopy)(T.Mg[:, a:b], T.Gt[:, W * tile:W * tile + W].indirect(T.OFF[:, a // 16:b // 16]), tok["list", tile], gz)
+                made.update({(tile, u): t for u in range(u0, u1)})
             elif what == "turn":
-                while any((k, u) not in made for u in range(u0, u1)):
-                    next(scalar)
-                t = turn(k, u0, u1, *[made[k, u] for u in range(u0, u1)])
-                turned.update({(k, u): t for u in range(u0, u1)})
-                for b in range(u0 // 4, (u1 + 3) // 4):
-                    toks = [turned[k, u] for u in range(4 * b, 4 * b + 4) if (k, u) in turned]
-                    if len(toks) == 4:
-                        done[k] = block(k, b, toks)
-            elif what == "places":
-                qs[q].wait_ge(crd[k], len(full))
-                tok[q, k] = (offs_s if q == "s" else offs_v)(slice(u0, u1))
-            elif what == "offsets":
-                while ("s", k) not in tok:
-                    next(scalar)
-                for i in range(u0, u1):
-                    tok["t", k] = offs_t(i, P[5 + k], 256 * (i - u0), tok["s", k], tok["v", k], off0)
+                tile, u0, u1 = arg
+                while any((tile, u) not in made for u in range(u0, u1)):
+                    yield False
+                a, b = 4096 * tile + 512 * u0, 4096 * tile + 512 * u1
+                need("v", *[made[tile, u] for u in range(u0, u1)])
+                t = did("v", V.transpose(T.Tt[:, a:b], T.Mg[:, a:b]))
+                first_order(tile, 16 * u0, 16 * u1, t, *tok["rw"])
+            elif what == "dist":
+                while arg[0] > 1 and ("list", arg[0] - 2) not in tok:
+                    yield False
+                dist(*arg)
+                offsets(*arg)
             elif what == "list":
-                t = vcopy(T.OFF[:, 256 * u0:256 * u1], P[5 + k][:, 0:256 * (u1 - u0)], tok["t", k])
-                tok.update({("off", i): t for i in range(u0, u1)})
-            elif k == 3:
-                c = u0
-                e = evac(0, c, [(P[2 + c], 0, 192, done[3][c])], [(0, 3, COPIERS["3"])])
-                send([msg(0, CC[c], 3, late[0][c], full)], *e[3])
+                while ("sum", arg[0]) not in tok:
+                    yield False
+                listed(*arg)
+            elif what == "order":
+                order(*arg, [vcopy, vcopy if plan is VPLAN else act])
             else:
-                c = u0
-                e = evac(0, c, [(P[c], 0, 192, max(done[1][c], done[2][c]))], [(0, 1, COPIERS["12"][0]), (1, 2, COPIERS["12"][1])])
-                e12.extend(e[1] + e[2])
-                if len(e12) == 8:
-                    send([msg(0, ALL, 1, T.sem.e0, h0), msg(0, ALL, 2, T.sem.e0, h1)], *e12)
-            yield what
+                {"run": later_order, "turn q": turn_q, "q": start}[what](*arg)
+            yield True
 
-    S.wait_ge(T.sem.dG, 16)
-    V.wait_ge(T.sem.dG, 16)
-    scalar = share("s", SPLAN)
-    for _ in share("v", VPLAN):
+    todo = [share("s", SPLAN), share("v", VPLAN)]
+    while todo:
+        todo = [p for p in todo if next(p, None) is not None]
+
+    for _ in share("v", TAIL):
         pass
-    for _ in scalar:
-        pass
-
-    mine = {}
-
-    def early_sum(o, c):
-        if o == 0:
-            i, t = scan(64, (P[4 + c], 0, 192, done[0][c]))
-            if c == 0:
-                V.wait_ge(T.sem.e0, len(full))
-                need("v", vtt(T.EA[:, 0, :], LD[0][:, 1, :], LD[0][:, 2, :], A.add))
-            need("v", t)
-            for ah in range(2):
-                r = slice(64 * ah, 64 * ah + 64)
-                e = did("v", V.tensor_tensor(T.EB[r, 0, CC[c]], T.EA[r, 0, CC[c]], part(i, 0, ah), A.add))
-            return e
-        V.wait_ge(early[c], len(full))
-        t = vtt(T.EA[:, 1, CC[c]], LD[1][:, 2, CC[c]], LD[1][:, 3, CC[c]], A.add)
-        return vtt(T.EB[:, 1, CC[c]], T.EA[:, 1, CC[c]], LD[1][:, 0, CC[c]], A.add, t, *mine[c])
-
-    banks = {1: [(6, 7, 0), (1, 2, 3)], 2: [(4, 5, 6), (7, 0, 1)]}
-    e0 = [early_sum(0, c) for c in range(2)]
-    for o in (1, 2):
-        f = []
-        for c in range(2):
-            e = e0[c] if o == 1 else early_sum(1, c)
-            V.wait_ge(late[o - 1][c], len(full))
-            s = vtt(T.SS[:, o - 1, CC[c]], T.EB[:, o - 1, CC[c]], LD[o - 1][:, 3 if o == 1 else 1, CC[c]], A.add, e)
-            need("v", s)
-            did("v", V.tensor_tensor(T.PC[:, 0, CC[c]], T.SS[:, o - 1, CC[c]], T.RT[:, CC[c]], A.mult))
-            hi = did("v", V.tensor_tensor(T.WW[:, CC[c]], T.SS[:, o - 1, CC[c]], T.RT[:, CC[c]], A.mult))
-            r = pieces(CC[c], hi, [vcopy, act])
-            bk = [P[b] for b in banks[o][c]]
-            fb = field(c, 128, 128, bk[0], 0, *r)
-            fa = [field(c, 0, 128, bk[1 + i], 0, xs=range(8 * i, 8 * i + 8)) for i in range(2)]
-            f.append(([(bk[0], 0, 192, fb)], [(bk[1 + i], 96 * i, 96 * i + 96, fa[i]) for i in range(2)]))
-
-        def first(c):
-            return evac(o, c, f[c][0], [(0, 2, COPIERS["fb"][0]), (1, 3, COPIERS["fb"][1])])
-
-        def second(c):
-            return evac(o, c, f[c][1], [(1, 1, COPIERS["fa"][0]), (0, 0, COPIERS["fa"][1])])
-
-        if o == 1:
-            for c in range(2):
-                e = first(c)
-                send([msg(o, CC[c], 2, early[c], h0), msg(o, CC[c], 3, early[c], h1)], *e[2], *e[3])
-                e = second(c)
-                send([msg(o, CC[c], 1, late[o][c], full)], *e[1])
-                mine[c] = e[0]
-        else:
-            ya = vtt(T.YA[:, :], T.SS[:, 0, :], T.SS[:, 1, :], A.add)
-            e = [first(c) for c in range(2)]
-            send([msg(o, ALL, 2, T.sem.e2, h0), msg(o, ALL, 3, T.sem.e2, h1)], *e[0][2], *e[0][3], *e[1][2], *e[1][3])
-            e = [second(c) for c in range(2)]
-            send([msg(o, ALL, 1, T.sem.a2, full)], *e[0][1], *e[1][1])
-            own = vtt(LD[o][:, 0, :], LD[o][:, 0, :], T.YA[:, :], A.add, ya, *e[0][0], *e[1][0])
-
-    V.wait_ge(T.sem.e2, len(full))
-    t = vtt(T.EA[:, 2, :], LD[2][:, 2, :], LD[2][:, 3, :], A.add)
-    e = vtt(T.EB[:, 2, :], T.EA[:, 2, :], LD[2][:, 0, :], A.add, t, own)
-    V.wait_ge(T.sem.a2, len(full))
-    for a2 in range(2):
-        y = vtt(T.YT[:, 32 * a2:32 * a2 + 32], T.EB[:, 2, a2:64:2], LD[2][:, 1, a2:64:2], A.add, e)
-    yt = mm(P[7][0:64, 256:384], T.YT[:, :], T.IP[:, :], True, True, y, ip)
-    yb = vcopy(T.YB[0:64, :], P[7][0:64, 256:384], yt)
-    need("y", yb)
-    g.sync.dma_start(T.y[0:64, :], T.YB[0:64, 0:64]).then_inc(T.sem.dY, 16)
-    need("s", yb)
-    g.scalar.dma_start(T.y[64:128, :], T.YB[0:64, 64:128]).then_inc(T.sem.dY, 16)
-    g.sync.wait_ge(T.sem.dY, 32)
+    finish()
+    Y.wait_ge(T.sem.dY, 64)
     need("g", *[(q, cnt[q]) for q in cnt])
     g.wait_ge(T.sem.sent, sent[0])

@@ -5,61 +5,68 @@ NR = 4
 F32, BF = "float32", "bfloat16"
 W = 4096 + 16
 TILES = [((0, 0), (0, 1)), ((2, 0), (2, 1)), ((1, 0), (3, 0)), ((1, 1), (3, 1))]
-SPLAN = [("dist", 1), ("gather", 0, 0, 2), ("dist", 2), ("gather", 0, 2, 4), ("dist", 3), ("gather", 1, 0, 6), ("gather", 2, 0, 4),
-         ("gather", 2, 4, 6), ("gather", 3, 0, 4), ("gather", 3, 4, 7)]
-VPLAN = [("gather", 0, 7, 8), ("list", 1), ("turn q",), ("gather", 0, 4, 7), ("list", 2), ("q",), ("turn", 0, 0, 8), ("list", 3),
-         ("gather", 1, 6, 8), ("turn", 1, 0, 8), ("gather", 2, 6, 8), ("turn", 2, 0, 4), ("turn", 2, 4, 8), ("gather", 3, 7, 8),
-         ("order", 0, 0, 0), ("run", 0, 1, 0, 0, 16), ("turn", 3, 0, 4), ("order", 0, 1, 0), ("turn", 3, 4, 8), ("run", 0, 2, 0, 0, 8)]
-TAIL = [("order", 1, 0, 0), ("run", 1, 1, 0, 0, 8), ("order", 1, 0, 1), ("run", 1, 1, 1, 8, 16), ("run", 0, 2, 0, 8, 16),
-        ("order", 1, 1, 0), ("run", 1, 2, 0, 0, 8), ("order", 1, 1, 1), ("run", 1, 2, 1, 8, 16),
-        ("order", 0, 2, 0), ("order", 1, 2, 0), ("order", 1, 2, 1)]
+CH = [[range(16)], [range(8), range(8, 16)]]
+BANK = [[[4, 5], [0, 1], [2, 3]], [[6, 7], [4, 5], [0, 1]]]
+SPLAN = [("dist", 1), ("gather", 0, 0, 2), ("dist", 2), ("gather", 0, 2, 4), ("dist", 3), ("gather", 1, 0, 3), ("gather", 1, 3, 6),
+         ("gather", 2, 0, 3), ("gather", 2, 3, 5), ("gather", 3, 0, 3), ("gather", 3, 3, 6), ("gather", 3, 6, 7)]
+VPLAN = [("sum", 1), ("gather", 0, 4, 6), ("list", 1), ("sum", 2), ("gather", 0, 6, 8), ("list", 2), ("sum", 3),
+         ("turn", 0, 4, 8), ("turn", 0, 0, 4), ("list", 3), ("turn q",), ("gather", 1, 6, 8), ("q",), ("first", 0), ("turn", 1, 0, 3),
+         ("gather", 2, 5, 8), ("turn", 1, 3, 8), ("first", 1), ("turn", 2, 0, 3), ("turn", 2, 5, 8), ("turn", 2, 3, 5), ("first", 2),
+         ("gather", 3, 7, 8), ("order", 0, 0, (0,), "vv"), ("run", 0, 1, 0), ("turn", 3, 0, 3), ("turn", 3, 3, 6), ("turn", 3, 6, 8),
+         ("first", 3), ("order", 0, 1, (0,), "vs"), ("run", 0, 2, 0)]
+TAIL = [("order", 1, 0, (0, 1), "vs"), ("run", 1, 1, 0), ("run", 1, 1, 1), ("add up", 0), ("order", 0, 2, (0,), ""),
+        ("order", 1, 1, (0,), "vs"), ("run", 1, 2, 0), ("order", 1, 1, (1,), "vs"), ("add up", 1), ("run", 1, 2, 1),
+        ("order", 1, 2, (0,), ""), ("order", 1, 2, (1,), ""), ("add up", 2)]
 SCRATCH = {
     "SP": ("dram", [4, 128, 2], "int32"), "RP": ("dram", [4, 128, 2], "int32"),
     "SQ": ("dram", [4, 128, 32], F32), "RQ": ("dram", [4, 128, 32], F32),
-    "SC": ("dram", [128, 1024], BF), "RC": ("dram", [128, 1024], BF),
-    "SB": ("dram", [2, 128, 512], BF), "RB": ("dram", [2, 128, 512], BF),
-    "SA": ("dram", [2, 128, 512], BF), "RA": ("dram", [2, 128, 512], BF),
+    "ST": ("dram", [6, 128, 512], BF), "RT": ("dram", [6, 128, 512], BF),
     "Gt": ("sbuf", [128, 4 * W], BF), "Mg": ("sbuf", [128, 16384], BF), "Tt": ("sbuf", [128, 16384], BF),
     "OFF": ("sbuf", [128, 1024], "uint16"), "DD": ("sbuf", [128, 16, 128], BF),
     "PLi": ("sbuf", [128, 128], "int32"), "PL": ("sbuf", [128, 128], BF),
-    "PT": ("sbuf", [128, 16], BF), "S0": ("sbuf", [128, 4], F32), "S1": ("sbuf", [128, 12], F32),
+    "PT": ("sbuf", [128, 16], BF), "S0": ("sbuf", [128, 6], F32), "I2": ("sbuf", [128, 128], BF), "EN": ("sbuf", [128, 2, 128], BF), "S1": ("sbuf", [128, 12], F32),
     "ONF": ("sbuf", [128, 128], F32), "IF": ("sbuf", [128, 128], F32), "IQ": ("sbuf", [128, 128], F32),
     "IB": ("sbuf", [128, 8, 16], BF), "I64": ("sbuf", [128, 128], BF), "IK": ("sbuf", [128, 128], BF),
     "E": ("sbuf", [128, 6, 4, 32], BF), "PM": ("sbuf", [128, 4, 2, 32], BF), "ZB": ("sbuf", [128, 256], BF),
-    "QN": ("sbuf", [128, 128], F32), "WQ": ("sbuf", [128, 64], F32),
-    "PC": ("sbuf", [128, 3, 64], BF), "R1": ("sbuf", [128, 64], F32), "RW": ("sbuf", [128, 2, 8, 64], BF),
-    "MK": ("sbuf", [128, 256], F32), "SCN": ("sbuf", [128, 6, 128], F32), "YA": ("sbuf", [128, 64], F32),
-    "YS": ("sbuf", [128, 64], F32), "YB": ("sbuf", [128, 64], F32), "LY": ("sbuf", [128, 4, 64], F32),
+    "QN": ("sbuf", [128, 128], F32),
+    "PC": ("sbuf", [128, 3, 256], BF), "R1": ("sbuf", [128, 64], F32), "RW": ("sbuf", [128, 2, 8, 64], BF),
+    "MK": ("sbuf", [128, 256], F32), "SCN": ("sbuf", [128, 3, 256], F32),
+    "YB": ("sbuf", [128, 64], F32), "LY": ("sbuf", [128, 4, 64], F32),
 }
 for _b in range(8):
     SCRATCH["P%d" % _b] = ("psum", [128, 512], F32)
-SEMAPHORES = ["qv", "qs", "qt", "qg", "dP", "dO", "dQ", "dC", "dA", "dL", "dN", "dG0", "dG1", "dG2", "dG3", "dY", "sent",
-              "aP", "aQ", "aC", "aA", "aB", "dB", "aY"]
+SEMAPHORES = ["qv", "qs", "qt", "qg", "dP", "dO", "dQ", "dL", "dN", "dG0", "dG1", "dG2", "dG3", "dY", "sent",
+              "dT1", "dT2", "dT3", "go", "aP", "aQ", "aG0", "aG1", "aG2", "aG3", "aG4", "aG5", "aY"]
 
 
 def bits(es):
     return sum(1 << e for e in es)
 
 
-def helpers(topo, core):
+def carrier(topo, core, tile, b):
+    ring = lambda c: topo.addr(c)[2]
+    if (tile + b) % 2 == 0:
+        return [c for c in topo.cores_of(core) if topo.die(c) == topo.die(core) and ring(c) != ring(core)][b]
     far = [c for c in topo.cores_of(core) if topo.die(c) != topo.die(core)]
-    return [far[0], [c for c in far if topo.addr(c)[2] != topo.addr(far[0])[2]][0]]
+    return [far[0], [c for c in far if ring(c) != ring(far[0])][0]][b]
 
 
-def helper_program(g, core, T, topo, rank, n):
-    to = T.cores[(rank + (3, 1)[n]) % NR]
-    rid, pid, _ = topo.addr(to)
-    g.wait_ge(T.sem.aA, (len(topo.engines(T.cores[rank], core)) - len(topo.engines(T.cores[rank], to))) // 2)
-    g.remote_dma(T.RA[n], T.SA[n], T.sem.aA, T.sem.sent, pid, rid, topo.mask(core, to))
-    g.wait_ge(T.sem.sent, len(topo.engines(core, to)))
+def helper_program(g, core, T, topo, rank):
+    for tile in (2, 3):
+        for b in range(2):
+            if carrier(topo, T.cores[rank], tile, b) == core:
+                to, a = T.cores[(rank - TILES[tile][b][0]) % NR], T.sem["aG%d" % (2 * tile - 2 + b)]
+                g.wait_ge(a, len(topo.engines(T.cores[rank], core)) - len(topo.engines(T.cores[rank], to)))
+                g.remote_dma(T.RT[2 * tile - 2 + b], T.ST[2 * tile - 2 + b], a, T.sem.sent, topo.addr(to)[1], topo.addr(to)[0], topo.mask(core, to))
+                g.wait_ge(T.sem.sent, len(topo.engines(core, to)))
 
 
 def rank_program(g, core, T, topo):
     rank = T.rank_of(core)
     if rank is None:
         for r, boss in enumerate(T.cores):
-            if core in helpers(topo, boss):
-                helper_program(g, core, T, topo, r, helpers(topo, boss).index(core))
+            if core in topo.cores_of(boss):
+                helper_program(g, core, T, topo, r)
         return
     A = AluOpType
     COPY, ABS = ActivationFunctionType.Copy, ActivationFunctionType.Abs
@@ -67,7 +74,7 @@ def rank_program(g, core, T, topo):
     sem = {"v": T.sem.qv, "s": T.sem.qs, "t": T.sem.qt, "g": T.sem.qg}
     cnt = {"v": 0, "s": 0, "t": 0, "g": 0}
     known = {q: {"v": 0, "s": 0, "t": 0, "g": 0} for q in qs}
-    sent = [0]
+    sent, tok = [0], {}
     V, S, Y = g.vector, g.scalar, g.sync
 
     def need(q, *toks):
@@ -134,18 +141,23 @@ def rank_program(g, core, T, topo):
         for u in us:
             dma(Y, T.Gt[rows(u), W * tile:W * tile + 4096], src, T.sem["dG%d" % tile])
 
+    def stage(tile):
+        for b, (k, c) in enumerate(TILES[tile]):
+            dma(Y, T.ST[2 * tile - 2 + b], T.green[rows(2 * who[NR - k] + c, 16), :], T.sem["dT%d" % tile])
+
+    def hand_on(tile, b, es):
+        n = 2 * tile - 2 + b
+        return [carrier(topo, core, tile, b)], [T.ST[n]], T.ST[n], T.sem["aG%d" % n], es
+
     dma(Y, T.SP[:, 0:64, :], T.px[:, :], T.sem.dP)
     dma(S, T.SP[:, 64:128, :], T.py[:, :], T.sem.dP)
     dma(Y, T.PLi[0:2, 0:64], T.px[rows(rank, 2), :], T.sem.dO)
     dma(S, T.PLi[0:2, 64:128], T.py[rows(rank, 2), :], T.sem.dO)
     dma(Y, T.SQ[:, 0:64, :], T.q[:, :], T.sem.dQ)
     dma(S, T.SQ[:, 64:128, :], T.refl[:, :], T.sem.dQ)
-    dma(Y, T.SC[:, :], T.green[rows(who[2]), :], T.sem.dC)
-    dma(S, T.QN[0:32, 0:64], T.q[rows(rank), :], T.sem.dN)
-    dma(S, T.QN[0:32, 64:128], T.refl[rows(rank), :], T.sem.dN)
-    for n, k in enumerate((3, 1)):
-        dma(Y, T.SA[n], T.green[rows(2 * who[k], 16), :], T.sem.dA)
     table(0, T.green[rows(rank), :], (0,))
+    stage(1)
+    stage(2)
 
     onf = fill(T.ONF[:, :], 1.0)
     idf = select(T.IF[:, :], T.ONF[:, :], [[-1, 128]], A.is_equal, 1, onf)
@@ -169,61 +181,79 @@ def rank_program(g, core, T, topo):
         for b in range(2):
             ee = vcopy(T.E[0:8, B, :, rows(b, 16)], T.E[0:8, 2 + 2 * b + B, :, 0:16], e)
     act(T.I64[:, :], T.IF[:, :], scale=64.0)
+    act(T.I2[:, :], T.IF[:, :], scale=2.0)
+    act(T.EN[0:8, :, :], T.E[0:8, 0:2, :, :], ee, scale=-1.0)
     ik = act(T.IK[:, :], T.IF[:, :], scale=4096.0)
 
     g.wait_ge(T.sem.dP, 32)
     send([([peer[k]], [T.RP[NR - k]], T.SP[who[k]], T.sem.aP, [full[quarter * k]]) for k in (1, 2, 3)])
-    g.wait_ge(T.sem.dQ, 32)
-    send([([peer[k]], [T.RQ[NR - k]], T.SQ[who[k]], T.sem.aQ, full[quarter * k:quarter * k + quarter]) for k in (1, 2, 3)])
-    g.wait_ge(T.sem.dC, 16)
-    send([([peer[2]], [T.RC[:, :]], T.SC[:, :], T.sem.aC, full)])
-    g.wait_ge(T.sem.dA, 32)
-    near = [e for e in topo.engines(core, helpers(topo, core)[0]) if e not in full]
-    send([([c], [T.SA[n]], T.SA[n], T.sem.aA, near[rows(n, len(near) // 2)]) for n, c in enumerate(helpers(topo, core))])
+    g.sem_inc(T.sem.go, 1)
+    Y.wait_ge(T.sem.go, 1)
+    table(0, T.green[rows(rank), :], (1, 2))
+    dma(Y, T.QN[0:32, 0:64], T.q[rows(rank), :], T.sem.dN)
+    dma(Y, T.QN[0:32, 64:128], T.refl[rows(rank), :], T.sem.dN)
     iq = select(T.IQ[:, :], T.ONF[:, :], [[-64, 2], [-1, 32], [-32, 2]], A.is_equal, 1)
     for q, o in ((Y, 0), (S, 64)):
         q.wait_ge(T.sem.aP, 3)
         dma(q, T.PLi[2:8, o:o + 64], T.RP[1:4, o:o + 64, :], T.sem.dL)
-    table(0, T.green[rows(rank), :], (1, 2, 3))
-    for n, k in enumerate((3, 1)):
-        dma(Y, T.SB[n], T.green[rows(2 * who[k] + 1, 16), :], T.sem.dB)
-    Y.wait_ge(T.sem.aQ, 3 * quarter)
-    for o in (0, 64):
-        dma(Y, T.QN[32:128, o:o + 64], T.RQ[1:4, o:o + 64, :], T.sem.dN)
-    g.wait_ge(T.sem.aC, len(full))
-    g.wait_ge(T.sem.dB, 32)
-    send([([peer[k]], [T.RB[n]], T.SB[n], T.sem.aB, full[rows(n, 2 * quarter)]) for n, k in enumerate((3, 1))])
-    for tile, src, a, n in ((1, T.RC[:, :], T.sem.aC, 1), (2, T.RA[0:2], T.sem.aA, 2), (3, T.RB[0:2], T.sem.aB, 1)):
-        Y.wait_ge(a, n * len(full))
-        table(tile, src)
+    table(0, T.green[rows(rank), :], (3,))
+    stage(3)
+    g.wait_ge(T.sem.aP, 3)
+    every = topo.engines(core, carrier(topo, core, 2, 0))
+    near = [e for e in every if e not in full]
+    for tile in (1, 2):
+        g.wait_ge(T.sem["dT%d" % tile], 32)
+    for b in range(2):
+        send([([peer[2]], [T.RT[b]], T.ST[b], T.sem["aG%d" % b], full), hand_on(2, b, near)])
+    g.wait_ge(T.sem.dQ, 32)
+    send([([peer[k]], [T.RQ[NR - k]], T.SQ[who[k]], T.sem.aQ, full[quarter * k:quarter * k + quarter]) for k in (1, 2, 3)])
+    g.wait_ge(T.sem.dT3, 32)
+    for b in range(2):
+        send([hand_on(3, b, near)])
+    for n in range(6):
+        Y.wait_ge(T.sem["aG%d" % n], len(full))
+        tile, b = 1 + n // 2, n % 2
+        for u in range(4):
+            dma(Y, T.Gt[rows(2 * u + b, 16), W * tile:W * tile + 4096], T.RT[n], T.sem["dG%d" % tile])
+        if n == 1:
+            Y.wait_ge(T.sem.aQ, 3 * quarter)
+            for o in (0, 64):
+                dma(Y, T.QN[32:128, o:o + 64], T.RQ[1:4, o:o + 64, :], T.sem.dN)
 
-    def sources(k, picks, c0, c1, out, *toks):
-        n = c1 - c0
+    def sources(k, picks, n, out, copy, *toks):
+        o0 = 0 if k == 2 else 4
         for xy in range(2):
             for r0, o, step in picks:
                 t = mm(P[4][0:64, o + xy:o + xy + step + 1:step], T.PL[0:k, rows(xy, 64)], T.IB[0:k, 0, r0:r0 + 2], True, True, *toks)
-        need("v", t)
-        for b in range(2):
-            t = did("v", V.tensor_copy(T.PT[0:64, 8 * b + c0:8 * b + c1], P[4][0:64, 8 * b + c0:8 * b + c1]))
+        yield
+        t = copy(T.PT[0:64, o0:o0 + 2 * n], P[4][0:64, 0:2 * n], t)
         for L in range(2):
             for jj in range(2):
                 for b in range(2):
-                    u = mm(P[4][rows(L, 64), 32 + n * jj:32 + n * jj + n], T.PM[0:64, 2 * jj + b, :, :], T.PT[0:64, 8 * b + c0:8 * b + c1],
+                    u = mm(P[4][rows(L, 64), 32 + n * jj:32 + n * jj + n], T.PM[0:64, 2 * jj + b, :, :], T.PT[0:64, o0 + n * b:o0 + n * b + n],
                            b == 0, b == 1, t, pm)
-        return vcopy(out, P[4][:, 32:32 + 2 * n], u), u
+        tok["src", k // 8] = copy(out, P[4][:, 32:32 + 2 * n], u)
+        tok["used"] = u
+        yield
 
     CL = [(P[0][:, 0:128], P[1][:, 0:128]), (P[2][:, 0:128], P[2][:, 128:256]), (P[2][:, 256:384], P[2][:, 384:512])]
     OB = [P[3], P[5], P[3], P[1]]
-    tok = {}
 
     def dist(tile):
         v = max(tile - 1, 0)
         need("s", tok["spread", v], tok["src", min(tile, 1)])
-        for xy in range(2):
+        for xy in range(2 if tile else 1):
             for jj in range(2):
                 o = 2 * jj + xy if tile == 0 else 6 * jj + 2 * tile - 2 + xy
                 tok["dist", tile, xy] = did("s", S.activation(T.DD[:, 4 * tile + 2 * xy + jj, :], CL[v][xy], ABS,
                                                               bias=(T.S1 if tile else T.S0)[:, o:o + 1], scale=-1.0))
+        if tile == 0:
+            need("v", tok["spread", 0], half)
+            for jj in range(2):
+                tok["dist", 0, 1] = did("v", V.tensor_scalar(T.DD[:, 2 + jj, :], CL[0][1], T.S0[:, 2 * jj + 1:2 * jj + 2], T.S0[:, 4 + jj:5 + jj],
+                                                             A.max, A.subtract))
+                for B in range(2):
+                    mm(OB[0][:, 128 * B + jj:128 * B + 128:2], T.EN[0:8, B, :], T.PL[0:8, 64:128], False, False)
 
     def selves(tile):
         mm(OB[tile][:, 0:256], T.IB[:, :, :], T.ZB[:, :], True, False, ib, ik, zb, tok.get(("list", tile - 2), ik), tok.get(("dist", tile - 2, 1), ik))
@@ -238,27 +268,29 @@ def rank_program(g, core, T, topo):
             selves(tile)
         for xy in range(2):
             for jj in range(2):
-                t = mm(OB[tile][:, jj:256:2], T.IB[:, :, :] if xy else T.I64[:, :], T.DD[:, 4 * tile + 2 * xy + jj, :], False, xy + jj == 2,
-                       tok["dist", tile, xy])
+                lhsT = (T.IB[:, :, :] if tile else T.I2[:, :]) if xy else T.I64[:, :]
+                t = mm(OB[tile][:, jj:256:2], lhsT, T.DD[:, 4 * tile + 2 * xy + jj, :], False, xy + jj == 2, tok["dist", tile, xy])
         tok["sum", tile] = t
 
     def listed(tile):
         tok["list", tile] = vcopy(T.OFF[:, rows(tile, 256)], OB[tile][:, 0:256], tok["sum", tile])
 
-    def pieces(w, cols, copiers, *toks):
-        r1 = T.R1[:, cols]
-        hi = vcopy(T.PC[:, 0, cols], w, *toks)
-        m = vtt(T.PC[:, 1, cols], w, T.PC[:, 0, cols], A.subtract, hi)
-        r = vtt(r1, w, T.PC[:, 0, cols], A.subtract)
-        lo = vtt(T.PC[:, 2, cols], r1, T.PC[:, 1, cols], A.subtract, m, r)
-        return [copiers[L](T.RW[rows(L, 64), B, 4 * L:4 * L + 3, cols], T.PC[rows(B, 64), :, cols], lo, rz) for B in range(2) for L in range(2)]
+    def pieces(w, cols, copiers, hi):
+        r1, at = T.R1[:, cols], slice(4 * cols.start + 3, 4 * cols.stop, 4)
+        m = vtt(T.PC[:, 1, at], w, T.PC[:, 0, at], A.subtract, hi)
+        r = vtt(r1, w, T.PC[:, 0, at], A.subtract)
+        lo = vtt(T.PC[:, 2, at], r1, T.PC[:, 1, at], A.subtract, m, r)
+        return [copiers[L](T.RW[rows(L, 64), B, 4 * L:4 * L + 3, cols], T.PC[rows(B, 64), :, at], lo, rz) for B in range(2) for L in range(2)]
 
     V.wait_ge(T.sem.dO, 32)
     pl = vcopy(T.PL[0:2, :], T.PLi[0:2, :])
-    tok["src", 0], used = sources(2, [(0, 0, 8)], 0, 2, T.S0[:, :], pl, ib)
+    for _ in sources(2, [(0, 0, 2)], 2, T.S0[:, 0:4], vcopy, pl, ib):
+        pass
+    need("v", tok["src", 0])
+    half = did("v", V.tensor_scalar(T.S0[:, 4:6], T.S0[:, 1:4:2], 0.5, None, A.mult))
     selves(0)
     V.wait_ge(T.sem.dL, 32)
-    pl = vcopy(T.PL[0:8, :], T.PLi[0:8, :], used)
+    pl = vcopy(T.PL[0:8, :], T.PLi[0:8, :], tok["used"])
 
     def spread(v):
         for xy in range(2):
@@ -269,9 +301,11 @@ def rank_program(g, core, T, topo):
 
     tok["spread", 0] = spread(0)
     dist(0)
-    tok["src", 1], used = sources(8, [(4, 2, 8), (2, 4, 2), (6, 12, 2)], 2, 8, T.S1[:, :], pl, tok["src", 0])
+    others = sources(8, [(4, 0, 6), (2, 2, 2), (6, 8, 2)], 6, T.S1[:, :], act, pl, tok["src", 0])
+    next(others)
     offsets(0)
     listed(0)
+    next(others)
     spread(1)
     tok["spread", 1] = tok["spread", 2] = spread(2)
 
@@ -282,12 +316,10 @@ def rank_program(g, core, T, topo):
                 tok["qt"] = mm(P[6][rows(B, 64), rows(i, 64)], T.QN[:, rows(i, 64)], T.IQ[:, rows(B, 64)], True, True, iq)
 
     def start():
-        t = vcopy(T.WQ[:, :], P[6][:, 0:64], tok["qt"])
+        tok["rw"] = pieces(P[6][:, 0:64], slice(0, 64), [gcopy(64)] * 2, vcopy(T.PC[:, 0, 3:256:4], P[6][:, 0:64], tok["qt"]))
         tok["mk"] = vcopy(T.MK[:, 3:256:4], P[6][:, 64:128], mk)
-        tok["rw"] = pieces(T.WQ[:, :], slice(0, 64), [gcopy(64)] * 2, t) + [tok["mk"]]
+        tok["rw"].append(tok["mk"])
 
-    CH = [[range(16)], [range(8), range(8, 16)]]
-    BANK = [[[4], [5], [4]], [[6, 7], [0, 1], [2, 3]]]
     field = {}
 
     def term(c, o, i, x, tile, b, t0, t1, first, last):
@@ -300,37 +332,38 @@ def rank_program(g, core, T, topo):
         for c in range(2):
             for i, xs in enumerate(CH[c]):
                 if ("open", c, i) not in tok:
-                    tok["open", c, i] = mm(P[BANK[c][0][i]][:, 0:8 * len(xs)], T.IB[:, :, :], T.ZB[:, 0:8 * len(xs)], True, False, tok["src", 1])
+                    tok["open", c, i] = mm(P[BANK[c][0][i]][:, 0:8 * len(xs)], T.IB[:, :, :], T.ZB[:, 0:8 * len(xs)], True, False, tok["src", 1], tok["list", 3])
                 todo = [(x, b) for x in xs for b in range(2) if TILES[tile][b][1] == c]
                 for x, b in todo:
                     field[c, 0, i] = term(c, 0, i, x, tile, b, t0, t1, False, tile == 2 + c and (x, b) == todo[-1])
 
-    def later_order(c, o, i, x0, x1):
+    def later_order(c, o, i):
         need("t", *tok["w", c, o, i])
         src = [(tile, b) for tile in range(4) for b in range(2) if TILES[tile][b][1] == c]
-        for x in range(x0, x1):
+        for x in CH[c][i]:
             for n, (tile, b) in enumerate(src):
                 field[c, o, i] = term(c, o, i, x, tile, b, 0, 128, n == 0, n == 3)
 
-    got, ya = [], {}
-
-    def order(c, o, i, copiers):
-        xs = CH[c][i]
-        a, b = 8 * xs[0], 8 * xs[-1] + 8
-        cols = slice(32 * c + 2 * xs[0], 32 * c + 2 * xs[-1] + 2)
-        need("v", field[c, o, i], tok["mk"])
-        t = did("v", V.tensor_tensor_scan(T.SCN[:, 3 * c + o, a:b], T.MK[:, 128 * c + a:128 * c + b], P[BANK[c][o][i]][:, 0:b - a], 0.0, A.mult, A.add))
+    def order(c, o, chunks, copiers):
+        for i in chunks:
+            a, b = 128 * c + 8 * CH[c][i][0], 128 * c + 8 * CH[c][i][-1] + 8
+            need("v", field[c, o, i], tok["mk"])
+            for out in (T.SCN[:, o, a:b], T.PC[:, 0, a:b])[:2 if o < 2 else 1]:
+                t = did("v", V.tensor_tensor_scan(out, T.MK[:, a:b], P[BANK[c][o][i]][:, 0:b - a], 0.0, A.mult, A.add))
+        tok["scan", o] = t
         if o < 2:
-            tok["w", c, o + 1, i] = pieces(T.SCN[:, 3 * c + o, a + 3:b:4], cols, copiers, t)
-        if o == 1:
-            ya[c, i] = vtt(T.YA[:, cols], T.SCN[:, 3 * c, a + 2:b:4], T.SCN[:, 3 * c + 1, a + 2:b:4], A.add)
-        if o == 2:
-            got.append(vtt(T.YS[:, cols], T.SCN[:, 3 * c + o, a + 2:b:4], T.YA[:, cols], A.add, t, ya[c, i]))
+            a = 128 * c + 8 * CH[c][chunks[0]][0]
+            t = pieces(T.SCN[:, o, a + 3:b:4], slice(a // 4, b // 4), copiers, t)
+            tok.update({("w", c, o + 1, i): t for i in chunks})
+
+    def add_up(o):
+        if o == 0:
+            mm(P[3][:, 0:64], T.IB[:, :, :], T.ZB[:, 0:64], True, False)
+        for B in range(2):
+            tok["y"] = mm(P[3][rows(B, 64), 0:64], T.SCN[:, o, 2:256:4], T.IF[:, rows(B, 64)], False, o == 2, tok["scan", o])
 
     def finish():
-        for B in range(2):
-            t = mm(P[5][rows(B, 64), 128:192], T.YS[:, :], T.IF[:, rows(B, 64)], True, True, *got)
-        t = vcopy(T.YB[:, :], P[5][:, 128:192], t)
+        t = vcopy(T.YB[:, :], P[3][:, 0:64], tok["y"])
         need("g", t)
         send([(peer[1:], [T.LY[:, NR - k, :] for k in (1, 2, 3)], T.YB[:, :], T.sem.aY, full)])
         need("s", t)
@@ -350,7 +383,7 @@ def rank_program(g, core, T, topo):
                 while ("list", tile) not in tok:
                     yield False
                 if (q, tile) not in loaded:
-                    qs[q].wait_ge(T.sem["dG%d" % tile], 64)
+                    qs[q].wait_ge(T.sem["dG%d" % tile], 128 if tile else 64)
                     loaded.add((q, tile))
                 a, b = 4096 * tile + 512 * u0, 4096 * tile + 512 * u1
                 t = (act if q == "s" else vcopy)(T.Mg[:, a:b], T.Gt[:, W * tile:W * tile + W].indirect(T.OFF[:, a // 16:b // 16]), tok["list", tile], gz)
@@ -361,21 +394,21 @@ def rank_program(g, core, T, topo):
                     yield False
                 a, b = 4096 * tile + 512 * u0, 4096 * tile + 512 * u1
                 need("v", *[made[tile, u] for u in range(u0, u1)])
-                t = did("v", V.transpose(T.Tt[:, a:b], T.Mg[:, a:b]))
-                first_order(tile, 16 * u0, 16 * u1, t, *tok["rw"])
+                tok["turn", tile] = did("v", V.transpose(T.Tt[:, a:b], T.Mg[:, a:b]))
+            elif what == "first":
+                first_order(arg[0], 0, 128, tok["turn", arg[0]], *tok["rw"])
             elif what == "dist":
-                while arg[0] > 1 and ("list", arg[0] - 2) not in tok:
-                    yield False
                 dist(*arg)
+            elif what == "sum":
+                while ("dist", arg[0], 1) not in tok:
+                    yield False
                 offsets(*arg)
             elif what == "list":
-                while ("sum", arg[0]) not in tok:
-                    yield False
                 listed(*arg)
             elif what == "order":
-                order(*arg, [vcopy, vcopy if plan is VPLAN else act])
+                order(*arg[:3], [{"v": vcopy, "s": act, "g": gcopy(32)}[w] for w in arg[3]])
             else:
-                {"run": later_order, "turn q": turn_q, "q": start}[what](*arg)
+                {"run": later_order, "turn q": turn_q, "q": start, "add up": add_up}[what](*arg)
             yield True
 
     todo = [share("s", SPLAN), share("v", VPLAN)]

from concourse.bass import DstId, RemoteDMATransfer
from concourse.mybir import AluOpType, ActivationFunctionType

NR = 4
F32, BF = "float32", "bfloat16"
W = 4096 + 16
TILES = [((0, 0), (0, 1)), ((2, 0), (2, 1)), ((1, 0), (3, 0)), ((1, 1), (3, 1))]
CH = [[range(16)], [range(8), range(8, 16)]]
BANK = [[[4, 5], [0, 1], [2, 3]], [[6, 7], [4, 5], [0, 1]]]
SPLAN = [("dist", 1), ("gather", 0, 0, 2), ("dist", 2), ("gather", 0, 2, 4), ("dist", 3), ("gather", 1, 0, 3), ("gather", 1, 3, 6),
         ("gather", 2, 0, 3), ("gather", 2, 3, 5), ("gather", 3, 0, 3), ("gather", 3, 3, 6), ("gather", 3, 6, 7)]
VPLAN = [("sum", 1), ("gather", 0, 4, 6), ("list", 1), ("sum", 2), ("gather", 0, 6, 8), ("list", 2), ("sum", 3),
         ("turn", 0, 4, 8), ("turn", 0, 0, 4), ("list", 3), ("turn q",), ("gather", 1, 6, 8), ("q",), ("first", 0), ("turn", 1, 0, 3),
         ("gather", 2, 5, 8), ("turn", 1, 3, 8), ("first", 1), ("turn", 2, 0, 3), ("turn", 2, 5, 8), ("turn", 2, 3, 5), ("first", 2),
         ("gather", 3, 7, 8), ("order", 0, 0, (0,), "vv"), ("run", 0, 1, 0), ("turn", 3, 0, 3), ("turn", 3, 3, 6), ("turn", 3, 6, 8),
         ("first", 3), ("order", 0, 1, (0,), "vs"), ("run", 0, 2, 0)]
TAIL = [("order", 1, 0, (0, 1), "vs"), ("run", 1, 1, 0), ("run", 1, 1, 1), ("add up", 0), ("order", 0, 2, (0,), ""),
        ("order", 1, 1, (0,), "vs"), ("run", 1, 2, 0), ("order", 1, 1, (1,), "vs"), ("add up", 1), ("run", 1, 2, 1),
        ("order", 1, 2, (0,), ""), ("order", 1, 2, (1,), ""), ("add up", 2)]
SCRATCH = {
    "SP": ("dram", [4, 128, 2], "int32"), "RP": ("dram", [4, 128, 2], "int32"),
    "SQ": ("dram", [4, 128, 32], F32), "RQ": ("dram", [4, 128, 32], F32),
    "ST": ("dram", [6, 128, 512], BF), "RT": ("dram", [6, 128, 512], BF),
    "Gt": ("sbuf", [128, 4 * W], BF), "Mg": ("sbuf", [128, 16384], BF), "Tt": ("sbuf", [128, 16384], BF),
    "OFF": ("sbuf", [128, 1024], "uint16"), "DD": ("sbuf", [128, 16, 128], BF),
    "PLi": ("sbuf", [128, 128], "int32"), "PL": ("sbuf", [128, 128], BF),
    "PT": ("sbuf", [128, 16], BF), "S0": ("sbuf", [128, 6], F32), "I2": ("sbuf", [128, 128], BF), "EN": ("sbuf", [128, 2, 128], BF), "S1": ("sbuf", [128, 12], F32),
    "ONF": ("sbuf", [128, 128], F32), "IF": ("sbuf", [128, 128], F32), "IQ": ("sbuf", [128, 128], F32),
    "IB": ("sbuf", [128, 8, 16], BF), "I64": ("sbuf", [128, 128], BF), "IK": ("sbuf", [128, 128], BF),
    "E": ("sbuf", [128, 6, 4, 32], BF), "PM": ("sbuf", [128, 4, 2, 32], BF), "ZB": ("sbuf", [128, 256], BF),
    "QN": ("sbuf", [128, 128], F32),
    "PC": ("sbuf", [128, 3, 256], BF), "R1": ("sbuf", [128, 64], F32), "RW": ("sbuf", [128, 2, 8, 64], BF),
    "MK": ("sbuf", [128, 256], F32), "SCN": ("sbuf", [128, 3, 256], F32),
    "YB": ("sbuf", [128, 64], F32), "LY": ("sbuf", [128, 4, 64], F32),
}
for _b in range(8):
    SCRATCH["P%d" % _b] = ("psum", [128, 512], F32)
SEMAPHORES = ["qv", "qs", "qt", "qg", "dP", "dO", "dQ", "dL", "dN", "dG0", "dG1", "dG2", "dG3", "dY", "sent",
              "dT1", "dT2", "dT3", "go", "aP", "aQ", "aG0", "aG1", "aG2", "aG3", "aG4", "aG5", "aY"]


def bits(es):
    return sum(1 << e for e in es)


def carrier(topo, core, tile, b):
    ring = lambda c: topo.addr(c)[2]
    if (tile + b) % 2 == 0:
        return [c for c in topo.cores_of(core) if topo.die(c) == topo.die(core) and ring(c) != ring(core)][b]
    far = [c for c in topo.cores_of(core) if topo.die(c) != topo.die(core)]
    return [far[0], [c for c in far if ring(c) != ring(far[0])][0]][b]


def helper_program(g, core, T, topo, rank):
    for tile in (2, 3):
        for b in range(2):
            if carrier(topo, T.cores[rank], tile, b) == core:
                to, a = T.cores[(rank - TILES[tile][b][0]) % NR], T.sem["aG%d" % (2 * tile - 2 + b)]
                g.wait_ge(a, len(topo.engines(T.cores[rank], core)) - len(topo.engines(T.cores[rank], to)))
                g.remote_dma(T.RT[2 * tile - 2 + b], T.ST[2 * tile - 2 + b], a, T.sem.sent, topo.addr(to)[1], topo.addr(to)[0], topo.mask(core, to))
                g.wait_ge(T.sem.sent, len(topo.engines(core, to)))


def rank_program(g, core, T, topo):
    rank = T.rank_of(core)
    if rank is None:
        for r, boss in enumerate(T.cores):
            if core in topo.cores_of(boss):
                helper_program(g, core, T, topo, r)
        return
    A = AluOpType
    COPY, ABS = ActivationFunctionType.Copy, ActivationFunctionType.Abs
    qs = {"v": g.vector, "s": g.scalar, "t": g.tensor, "g": g, "y": g.sync}
    sem = {"v": T.sem.qv, "s": T.sem.qs, "t": T.sem.qt, "g": T.sem.qg}
    cnt = {"v": 0, "s": 0, "t": 0, "g": 0}
    known = {q: {"v": 0, "s": 0, "t": 0, "g": 0} for q in qs}
    sent, tok = [0], {}
    V, S, Y = g.vector, g.scalar, g.sync

    def need(q, *toks):
        top = {}
        for tk in toks:
            top[tk[0]] = max(top.get(tk[0], 0), tk[1])
        for p, n in top.items():
            if known[q][p] < n:
                qs[q].wait_ge(sem[p], n)
                known[q][p] = n

    def did(q, inst):
        inst.then_inc(sem[q], 1)
        cnt[q] += 1
        return (q, cnt[q])

    def fill(ap, value):
        return did("v", V.memset(ap, value))

    def vcopy(out, in_, *toks):
        need("v", *toks)
        return did("v", V.tensor_copy(out, in_))

    def vtt(out, a, b, op, *toks):
        need("v", *toks)
        return did("v", V.tensor_tensor(out, a, b, op))

    def act(out, in_, *toks, scale=1.0):
        need("s", *toks)
        return did("s", S.activation(out, in_, COPY, scale=scale))

    def mm(out, lhsT, rhs, start, stop, *toks):
        need("t", *toks)
        return did("t", g.tensor.matmul(out, lhsT, rhs, start, stop))

    def select(out, in_, pattern, op, cm, *toks):
        need("g", *toks)
        return did("g", g.affine_select(out, in_, pattern, op, 0.0, 0, cm))

    def gcopy(n):
        return lambda out, in_, *toks: select(out, in_, [[0, 3], [0, n]], A.is_ge, 0, ("g", cnt["g"]), *toks)

    def dma(q, out, in_, s):
        q.dma_start(out, in_).then_inc(s, 16)

    P = [T["P%d" % b] for b in range(8)]
    who = [(rank + k) % NR for k in range(NR)]
    full = topo.engines(core, T.cores[who[1]])
    quarter = len(full) // 4
    peer = [T.cores[r] for r in who]

    def send(parts):
        tr = []
        for cs, dsts, src, rs, es in parts:
            ids = [DstId(rid=topo.addr(c)[0], pnc=topo.addr(c)[1]) for c in cs]
            tr.append(RemoteDMATransfer(dst_ids=ids, dma_engine_mask=bits(es), remote_sem=rs, srcs=[src], dsts=dsts))
            sent[0] += len(es)
        g.remote_dma_fused(tr, local_sem=T.sem.sent)

    def rows(k, n=32):
        return slice(n * k, n * k + n)

    def table(tile, src, us=range(4)):
        for u in us:
            dma(Y, T.Gt[rows(u), W * tile:W * tile + 4096], src, T.sem["dG%d" % tile])

    def stage(tile):
        for b, (k, c) in enumerate(TILES[tile]):
            dma(Y, T.ST[2 * tile - 2 + b], T.green[rows(2 * who[NR - k] + c, 16), :], T.sem["dT%d" % tile])

    def hand_on(tile, b, es):
        n = 2 * tile - 2 + b
        return [carrier(topo, core, tile, b)], [T.ST[n]], T.ST[n], T.sem["aG%d" % n], es

    dma(Y, T.SP[:, 0:64, :], T.px[:, :], T.sem.dP)
    dma(S, T.SP[:, 64:128, :], T.py[:, :], T.sem.dP)
    dma(Y, T.PLi[0:2, 0:64], T.px[rows(rank, 2), :], T.sem.dO)
    dma(S, T.PLi[0:2, 64:128], T.py[rows(rank, 2), :], T.sem.dO)
    dma(Y, T.SQ[:, 0:64, :], T.q[:, :], T.sem.dQ)
    dma(S, T.SQ[:, 64:128, :], T.refl[:, :], T.sem.dQ)
    table(0, T.green[rows(rank), :], (0,))
    stage(1)
    stage(2)

    onf = fill(T.ONF[:, :], 1.0)
    idf = select(T.IF[:, :], T.ONF[:, :], [[-1, 128]], A.is_equal, 1, onf)
    pm = fill(T.PM[0:64, :, :, :], 0.0)
    for t in range(4):
        gz = fill(T.Gt[:, W * t + 4096:W * t + W], 0.0)
    zb = fill(T.ZB[:, :], 0.0)
    mk = fill(T.MK[:, :], 1.0)
    rz = fill(T.RW[:, :, :, :], 0.0)
    need("v", mk)
    mk = fill(T.MK[:, 0:256:4], 0.0)
    ib = vcopy(T.IB[:, :, :], T.IF[:, :], idf)
    need("v", pm, ib)
    for jj in range(2):
        for b in range(2):
            pm = vcopy(T.PM[0:64, 2 * jj + b, :, rows(b, 16)], T.IB[0:64, jj:4:2, :])
    for c in range(2):
        for k in range(4):
            e = act(T.E[0:8, 2 + 2 * c + k // 2, rows(k % 2, 2), :], T.ONF[0:8, 0:64], idf, scale=T.IF[0:8, 2 * k + c:2 * k + c + 1])
    for B in range(2):
        for b in range(2):
            ee = vcopy(T.E[0:8, B, :, rows(b, 16)], T.E[0:8, 2 + 2 * b + B, :, 0:16], e)
    act(T.I64[:, :], T.IF[:, :], scale=64.0)
    act(T.I2[:, :], T.IF[:, :], scale=2.0)
    act(T.EN[0:8, :, :], T.E[0:8, 0:2, :, :], ee, scale=-1.0)
    ik = act(T.IK[:, :], T.IF[:, :], scale=4096.0)

    g.wait_ge(T.sem.dP, 32)
    send([([peer[k]], [T.RP[NR - k]], T.SP[who[k]], T.sem.aP, [full[quarter * k]]) for k in (1, 2, 3)])
    g.sem_inc(T.sem.go, 1)
    Y.wait_ge(T.sem.go, 1)
    table(0, T.green[rows(rank), :], (1, 2))
    dma(Y, T.QN[0:32, 0:64], T.q[rows(rank), :], T.sem.dN)
    dma(Y, T.QN[0:32, 64:128], T.refl[rows(rank), :], T.sem.dN)
    iq = select(T.IQ[:, :], T.ONF[:, :], [[-64, 2], [-1, 32], [-32, 2]], A.is_equal, 1)
    for q, o in ((Y, 0), (S, 64)):
        q.wait_ge(T.sem.aP, 3)
        dma(q, T.PLi[2:8, o:o + 64], T.RP[1:4, o:o + 64, :], T.sem.dL)
    table(0, T.green[rows(rank), :], (3,))
    stage(3)
    g.wait_ge(T.sem.aP, 3)
    every = topo.engines(core, carrier(topo, core, 2, 0))
    near = [e for e in every if e not in full]
    for tile in (1, 2):
        g.wait_ge(T.sem["dT%d" % tile], 32)
    for b in range(2):
        send([([peer[2]], [T.RT[b]], T.ST[b], T.sem["aG%d" % b], full), hand_on(2, b, near)])
    g.wait_ge(T.sem.dQ, 32)
    send([([peer[k]], [T.RQ[NR - k]], T.SQ[who[k]], T.sem.aQ, full[quarter * k:quarter * k + quarter]) for k in (1, 2, 3)])
    g.wait_ge(T.sem.dT3, 32)
    for b in range(2):
        send([hand_on(3, b, near)])
    for n in range(6):
        Y.wait_ge(T.sem["aG%d" % n], len(full))
        tile, b = 1 + n // 2, n % 2
        for u in range(4):
            dma(Y, T.Gt[rows(2 * u + b, 16), W * tile:W * tile + 4096], T.RT[n], T.sem["dG%d" % tile])
        if n == 1:
            Y.wait_ge(T.sem.aQ, 3 * quarter)
            for o in (0, 64):
                dma(Y, T.QN[32:128, o:o + 64], T.RQ[1:4, o:o + 64, :], T.sem.dN)

    def sources(k, picks, n, out, copy, *toks):
        o0 = 0 if k == 2 else 4
        for xy in range(2):
            for r0, o, step in picks:
                t = mm(P[4][0:64, o + xy:o + xy + step + 1:step], T.PL[0:k, rows(xy, 64)], T.IB[0:k, 0, r0:r0 + 2], True, True, *toks)
        yield
        t = copy(T.PT[0:64, o0:o0 + 2 * n], P[4][0:64, 0:2 * n], t)
        for L in range(2):
            for jj in range(2):
                for b in range(2):
                    u = mm(P[4][rows(L, 64), 32 + n * jj:32 + n * jj + n], T.PM[0:64, 2 * jj + b, :, :], T.PT[0:64, o0 + n * b:o0 + n * b + n],
                           b == 0, b == 1, t, pm)
        tok["src", k // 8] = copy(out, P[4][:, 32:32 + 2 * n], u)
        tok["used"] = u
        yield

    CL = [(P[0][:, 0:128], P[1][:, 0:128]), (P[2][:, 0:128], P[2][:, 128:256]), (P[2][:, 256:384], P[2][:, 384:512])]
    OB = [P[3], P[5], P[3], P[1]]

    def dist(tile):
        v = max(tile - 1, 0)
        need("s", tok["spread", v], tok["src", min(tile, 1)])
        for xy in range(2 if tile else 1):
            for jj in range(2):
                o = 2 * jj + xy if tile == 0 else 6 * jj + 2 * tile - 2 + xy
                tok["dist", tile, xy] = did("s", S.activation(T.DD[:, 4 * tile + 2 * xy + jj, :], CL[v][xy], ABS,
                                                              bias=(T.S1 if tile else T.S0)[:, o:o + 1], scale=-1.0))
        if tile == 0:
            need("v", tok["spread", 0], half)
            for jj in range(2):
                tok["dist", 0, 1] = did("v", V.tensor_scalar(T.DD[:, 2 + jj, :], CL[0][1], T.S0[:, 2 * jj + 1:2 * jj + 2], T.S0[:, 4 + jj:5 + jj],
                                                             A.max, A.subtract))
                for B in range(2):
                    mm(OB[0][:, 128 * B + jj:128 * B + 128:2], T.EN[0:8, B, :], T.PL[0:8, 64:128], False, False)

    def selves(tile):
        mm(OB[tile][:, 0:256], T.IB[:, :, :], T.ZB[:, :], True, False, ib, ik, zb, tok.get(("list", tile - 2), ik), tok.get(("dist", tile - 2, 1), ik))
        for jj in range(2):
            for b, (k, _) in enumerate(TILES[tile]):
                for h in range(2):
                    o = 2 * (64 * (k // 2) + 32 * h + 16 * jj) + jj
                    mm(OB[tile][:, o:o + 31:2], T.IK[:, :], T.IB[:, 4 * (k % 2) + 2 * h + b, :], False, False)

    def offsets(tile):
        if tile:
            selves(tile)
        for xy in range(2):
            for jj in range(2):
                lhsT = (T.IB[:, :, :] if tile else T.I2[:, :]) if xy else T.I64[:, :]
                t = mm(OB[tile][:, jj:256:2], lhsT, T.DD[:, 4 * tile + 2 * xy + jj, :], False, xy + jj == 2, tok["dist", tile, xy])
        tok["sum", tile] = t

    def listed(tile):
        tok["list", tile] = vcopy(T.OFF[:, rows(tile, 256)], OB[tile][:, 0:256], tok["sum", tile])

    def pieces(w, cols, copiers, hi):
        r1, at = T.R1[:, cols], slice(4 * cols.start + 3, 4 * cols.stop, 4)
        m = vtt(T.PC[:, 1, at], w, T.PC[:, 0, at], A.subtract, hi)
        r = vtt(r1, w, T.PC[:, 0, at], A.subtract)
        lo = vtt(T.PC[:, 2, at], r1, T.PC[:, 1, at], A.subtract, m, r)
        return [copiers[L](T.RW[rows(L, 64), B, 4 * L:4 * L + 3, cols], T.PC[rows(B, 64), :, at], lo, rz) for B in range(2) for L in range(2)]

    V.wait_ge(T.sem.dO, 32)
    pl = vcopy(T.PL[0:2, :], T.PLi[0:2, :])
    for _ in sources(2, [(0, 0, 2)], 2, T.S0[:, 0:4], vcopy, pl, ib):
        pass
    need("v", tok["src", 0])
    half = did("v", V.tensor_scalar(T.S0[:, 4:6], T.S0[:, 1:4:2], 0.5, None, A.mult))
    selves(0)
    V.wait_ge(T.sem.dL, 32)
    pl = vcopy(T.PL[0:8, :], T.PLi[0:8, :], tok["used"])

    def spread(v):
        for xy in range(2):
            for B in range(2):
                bank, o = (P[2], 256 * v - 256 + 128 * xy + 64 * B) if v else (P[xy], 64 * B)
                t = mm(bank[:, o:o + 64], T.E[0:8, 2 * v + B, :, :], T.PL[0:8, rows(xy, 64)], True, True, pl, ee)
        return t

    tok["spread", 0] = spread(0)
    dist(0)
    others = sources(8, [(4, 0, 6), (2, 2, 2), (6, 8, 2)], 6, T.S1[:, :], act, pl, tok["src", 0])
    next(others)
    offsets(0)
    listed(0)
    next(others)
    spread(1)
    tok["spread", 1] = tok["spread", 2] = spread(2)

    def turn_q():
        g.tensor.wait_ge(T.sem.dN, 64)
        for i in range(2):
            for B in range(2):
                tok["qt"] = mm(P[6][rows(B, 64), rows(i, 64)], T.QN[:, rows(i, 64)], T.IQ[:, rows(B, 64)], True, True, iq)

    def start():
        tok["rw"] = pieces(P[6][:, 0:64], slice(0, 64), [gcopy(64)] * 2, vcopy(T.PC[:, 0, 3:256:4], P[6][:, 0:64], tok["qt"]))
        tok["mk"] = vcopy(T.MK[:, 3:256:4], P[6][:, 64:128], mk)
        tok["rw"].append(tok["mk"])

    field = {}

    def term(c, o, i, x, tile, b, t0, t1, first, last):
        k, xl = TILES[tile][b][0], x - CH[c][i][0]
        a = 4096 * tile + 16 * b + x
        return mm(P[BANK[c][o][i]][t0:t1, 8 * xl:8 * xl + 8], T.Tt[:, a + 32 * t0:a + 32 * t1 - 31:32], T.RW[:, k // 2, :, 32 * c + 2 * x + k % 2], first, last)

    def first_order(tile, t0, t1, *toks):
        need("t", *toks)
        for c in range(2):
            for i, xs in enumerate(CH[c]):
                if ("open", c, i) not in tok:
                    tok["open", c, i] = mm(P[BANK[c][0][i]][:, 0:8 * len(xs)], T.IB[:, :, :], T.ZB[:, 0:8 * len(xs)], True, False, tok["src", 1], tok["list", 3])
                todo = [(x, b) for x in xs for b in range(2) if TILES[tile][b][1] == c]
                for x, b in todo:
                    field[c, 0, i] = term(c, 0, i, x, tile, b, t0, t1, False, tile == 2 + c and (x, b) == todo[-1])

    def later_order(c, o, i):
        need("t", *tok["w", c, o, i])
        src = [(tile, b) for tile in range(4) for b in range(2) if TILES[tile][b][1] == c]
        for x in CH[c][i]:
            for n, (tile, b) in enumerate(src):
                field[c, o, i] = term(c, o, i, x, tile, b, 0, 128, n == 0, n == 3)

    def order(c, o, chunks, copiers):
        for i in chunks:
            a, b = 128 * c + 8 * CH[c][i][0], 128 * c + 8 * CH[c][i][-1] + 8
            need("v", field[c, o, i], tok["mk"])
            for out in (T.SCN[:, o, a:b], T.PC[:, 0, a:b])[:2 if o < 2 else 1]:
                t = did("v", V.tensor_tensor_scan(out, T.MK[:, a:b], P[BANK[c][o][i]][:, 0:b - a], 0.0, A.mult, A.add))
        tok["scan", o] = t
        if o < 2:
            a = 128 * c + 8 * CH[c][chunks[0]][0]
            t = pieces(T.SCN[:, o, a + 3:b:4], slice(a // 4, b // 4), copiers, t)
            tok.update({("w", c, o + 1, i): t for i in chunks})

    def add_up(o):
        if o == 0:
            mm(P[3][:, 0:64], T.IB[:, :, :], T.ZB[:, 0:64], True, False)
        for B in range(2):
            tok["y"] = mm(P[3][rows(B, 64), 0:64], T.SCN[:, o, 2:256:4], T.IF[:, rows(B, 64)], False, o == 2, tok["scan", o])

    def finish():
        t = vcopy(T.YB[:, :], P[3][:, 0:64], tok["y"])
        need("g", t)
        send([(peer[1:], [T.LY[:, NR - k, :] for k in (1, 2, 3)], T.YB[:, :], T.sem.aY, full)])
        need("s", t)
        dma(S, T.y[rows(rank), :], T.YB[0:64:2, :], T.sem.dY)
        for q in (Y, S):
            q.wait_ge(T.sem.aY, 3 * len(full))
        for k in (1, 2, 3):
            B, L = divmod(NR - k, 2)
            dma((Y, S)[k == 2], T.y[rows(who[k]), :], T.LY[64 * B + L:64 * B + 64:2, k, :], T.sem.dY)

    made, loaded = {}, set()

    def share(q, plan):
        for what, *arg in plan:
            if what == "gather":
                tile, u0, u1 = arg
                while ("list", tile) not in tok:
                    yield False
                if (q, tile) not in loaded:
                    qs[q].wait_ge(T.sem["dG%d" % tile], 128 if tile else 64)
                    loaded.add((q, tile))
                a, b = 4096 * tile + 512 * u0, 4096 * tile + 512 * u1
                t = (act if q == "s" else vcopy)(T.Mg[:, a:b], T.Gt[:, W * tile:W * tile + W].indirect(T.OFF[:, a // 16:b // 16]), tok["list", tile], gz)
                made.update({(tile, u): t for u in range(u0, u1)})
            elif what == "turn":
                tile, u0, u1 = arg
                while any((tile, u) not in made for u in range(u0, u1)):
                    yield False
                a, b = 4096 * tile + 512 * u0, 4096 * tile + 512 * u1
                need("v", *[made[tile, u] for u in range(u0, u1)])
                tok["turn", tile] = did("v", V.transpose(T.Tt[:, a:b], T.Mg[:, a:b]))
            elif what == "first":
                first_order(arg[0], 0, 128, tok["turn", arg[0]], *tok["rw"])
            elif what == "dist":
                dist(*arg)
            elif what == "sum":
                while ("dist", arg[0], 1) not in tok:
                    yield False
                offsets(*arg)
            elif what == "list":
                listed(*arg)
            elif what == "order":
                order(*arg[:3], [{"v": vcopy, "s": act, "g": gcopy(32)}[w] for w in arg[3]])
            else:
                {"run": later_order, "turn q": turn_q, "q": start, "add up": add_up}[what](*arg)
            yield True

    todo = [share("s", SPLAN), share("v", VPLAN)]
    while todo:
        todo = [p for p in todo if next(p, None) is not None]

    for _ in share("v", TAIL):
        pass
    finish()
    Y.wait_ge(T.sem.dY, 64)
    need("g", *[(q, cnt[q]) for q in cnt])
    g.wait_ge(T.sem.sent, sent[0])
